import numpy as np
import ml_dtypes


def mxq(x, axis, fmt="e4m3"):
    dtype, down = {"e4m3": (ml_dtypes.float8_e4m3fn, 7), "e5m2": (ml_dtypes.float8_e5m2, 14)}[fmt]
    v = np.moveaxis(np.asarray(x, np.float32).astype(ml_dtypes.bfloat16).astype(np.float64), axis, -1)
    blocks = v.reshape(v.shape[:-1] + (-1, 32))
    amax = np.abs(blocks).max(-1, keepdims=True)
    byte = np.maximum(np.where(amax > 0, np.frexp(amax)[1] - 1 + 127, 0) - down, 1)
    scale = np.exp2(byte - 127.0)
    codes = (blocks / scale).astype(np.float32).astype(dtype).astype(np.float64)
    return np.moveaxis((codes * scale).reshape(v.shape), -1, axis)


WIDE = False


def mx_kscale(k):
    if not WIDE:
        return np.ones(k)
    levels = np.array([10, -10, 5, -5, 0])
    if k % 512:
        return np.exp2(np.random.permutation(np.resize(levels, k // 32))).repeat(32)
    a = np.empty((k // 512, 16))
    for p in range(k // 512):
        a[p, :8] = np.random.permutation(np.resize(levels, 8))
        for g in range(8):
            far = levels[np.abs(levels - a[p, g]) >= 10]
            a[p, g + 8] = far[np.random.randint(len(far))]
    return np.exp2(a.ravel()).repeat(32)


def f64(x):
    return np.asarray(x).astype(np.float64)


def striped(idx):
    return np.tile(idx.reshape(-1, 16).T, (8, 1)).astype(np.uint16)


def unstriped(offs):
    return offs[:16].T.reshape(-1).astype(np.int64)


E2M1 = np.array([0.0, 0.5, 1.0, 1.5, 2.0, 3.0, 4.0, 6.0, -0.0, -0.5, -1.0, -1.5, -2.0, -3.0, -4.0, -6.0])


def pack_weight(w, fmt):
    k, n = w.shape
    w = f64(np.asarray(w, np.float32).astype(ml_dtypes.bfloat16)).reshape(k // 32, 32, n)
    amax = np.abs(w).max(1)
    if fmt == "e4m3":
        byte = np.frexp(amax)[1] - 1 + 127 - 7
    else:
        mant, ex = np.frexp(amax / 6.0)
        byte = np.where(mant > 0.5, ex, ex - 1) + 127
    byte = np.clip(np.where(amax > 0, byte, 1), 1, 254)
    scaled = (w * np.exp2(127.0 - byte)[:, None, :]).reshape(k, n).astype(np.float32)
    by_word = np.ascontiguousarray(scaled.reshape(k // 512, 128, 4, n).transpose(0, 1, 3, 2))
    if fmt == "e4m3":
        words = by_word.astype(ml_dtypes.float8_e4m3fn).view(np.uint8)
    else:
        c = by_word.astype(ml_dtypes.float4_e2m1fn).view(np.uint8) & 0xF
        words = (c[..., 0::2] | (c[..., 1::2] << 4)).reshape(k // 512, 128, 2 * n)
    return np.ascontiguousarray(words), np.ascontiguousarray(byte.astype(np.uint8).reshape(k // 512, 16, n))


def unpack_weight(words, scales, fmt):
    g, _, n = scales.shape
    words = np.ascontiguousarray(words).reshape(g, 128, n, -1)
    if fmt == "e4m3":
        vals = words.view(ml_dtypes.float8_e4m3fn).astype(np.float64)
    else:
        nib = np.empty((g, 128, n, 4), np.uint8)
        nib[..., 0::2] = words & 0xF
        nib[..., 1::2] = words >> 4
        vals = E2M1[nib]
    vals = vals * np.repeat(np.exp2(scales.astype(np.float64) - 127.0), 8, axis=1)[..., None]
    return vals.transpose(0, 1, 3, 2).reshape(g * 512, n)


def gelu(v):
    return 0.5 * v * (1.0 + np.tanh(np.sqrt(2.0 / np.pi) * (v + 0.044715 * v**3)))


def bf(x):
    return np.asarray(x, np.float32).astype(ml_dtypes.bfloat16)


def planes(Y):
    n, m = Y.shape
    b = f64(bf(Y)).reshape(n // 32, 32, m)
    amax = np.abs(b).max(1)
    byte = np.clip(np.where(amax > 0, np.frexp(amax)[1] - 1 + 127 - 7, 1), 1, 254)
    codes = (b * np.exp2(127.0 - byte)[:, None, :]).reshape(n, m).astype(np.float32).astype(ml_dtypes.float8_e4m3fn).view(np.uint8)
    words = codes.reshape(n // 512, 128, 4, m).transpose(0, 1, 3, 2)
    return np.ascontiguousarray(words), np.ascontiguousarray(byte.astype(np.uint8).reshape(n // 512, 16, m))


T, S, P, P2, K, H, M, N = 4096, 2048, 1024, 512, 512, 1024, 512, 1024

def setup_inputs():
    n = np.random.standard_normal
    s = mx_kscale(K)[:, None]
    u = mx_kscale(H)[:, None]
    u2 = mx_kscale(M)[:, None]
    cn = np.exp(0.8 * n(N))[None, :]
    tab_words, tab_scales = pack_weight(n((K, T)) * s, "e4m3")
    w2_words, w2_scales = pack_weight(n((H, M)) * 2.0 / np.sqrt(H) / u, "e2m1")
    w4_words, w4_scales = pack_weight(n((H, N)) * 0.8 / np.sqrt(H) / u * cn, "e4m3")
    return {
        "tab_words": tab_words, "tab_scales": tab_scales,
        "offs": striped(np.random.permutation(T)[:S]),
        "pos1": striped(np.random.permutation(S)[:P]),
        "pos2": striped(np.random.permutation(S)[:P]),
        "pos3": striped(np.random.permutation(P)[:P2]),
        "pos4": striped(np.random.permutation(S)[:P2]),
        "w1": (n((K, H)) * 1.5 / np.sqrt(K) / s).astype(np.float32),
        "gain": (np.exp(0.3 * n(H)) * u[:, 0]).astype(np.float32),
        "w2_words": w2_words, "w2_scales": w2_scales,
        "gain2": (np.exp(0.3 * n(M)) * u2[:, 0]).astype(np.float32),
        "w3": (n((M, N)) * 1.2 / np.sqrt(M) / u2 * cn).astype(np.float32),
        "w4_words": w4_words, "w4_scales": w4_scales,
    }

def reference(tab_words, tab_scales, offs, pos1, pos2, pos3, pos4, w1, gain, w2_words, w2_scales, gain2, w3, w4_words, w4_scales):
    v = unpack_weight(tab_words, tab_scales, "e4m3")[:, unstriped(offs)]
    w2 = unpack_weight(w2_words, w2_scales, "e2m1")
    w4 = unpack_weight(w4_words, w4_scales, "e4m3")
    h = f64(gain)[:, None] * np.tanh(mxq(f64(w1), 0, "e4m3").T @ v)
    a1 = h[:, unstriped(pos1)] - h[:, unstriped(pos2)]
    a2 = np.minimum(a1[:, unstriped(pos3)], h[:, unstriped(pos4)])
    qa = mxq(a2, 0, "e4m3")
    d = f64(gain2)[:, None] * np.tanh(w2.T @ qa)
    y = mxq(f64(w3), 0, "e4m3").T @ mxq(d, 0, "e4m3") + w4.T @ qa
    words, scales = planes(y)
    return y, words, scales

@@ -1,0 +1,289 @@
+from contextlib import ExitStack
+
+import concourse.mybir as mybir
+
+F32 = mybir.dt.float32
+BF16 = mybir.dt.bfloat16
+I32 = mybir.dt.int32
+U32 = mybir.dt.uint32
+U16 = mybir.dt.uint16
+U8 = mybir.dt.uint8
+FP8X4 = mybir.dt.float8_e4m3fn_x4
+FP4X4 = mybir.dt.float4_e2m1fn_x4
+ACT = mybir.ActivationFunctionType
+ALU = mybir.AluOpType
+
+T, S, PAIRS, KEPT = 4096, 2048, 1024, 512
+K, H, M, N = 512, 1024, 512, 1024
+P = 128
+BANK = 512
+UNIT = 128
+UNITS = KEPT // UNIT
+FLOPS = 2 * (K * H * S + H * M * KEPT + M * N * KEPT + H * N * KEPT)
+
+
+def tile_list_spatter_pair_features_kernel(
+    tc, tab_words, tab_scales, offs, pos1, pos2, pos3, pos4, w1, gain, w2_words, w2_scales, gain2, w3,
+    w4_words, w4_scales, out_0, out_1, out_2,
+):
+    nc = tc.nc
+    with ExitStack() as ctx:
+        keep = ctx.enter_context(tc.tile_pool(name="keep", bufs=1))
+        ring = ctx.enter_context(tc.tile_pool(name="ring", bufs=2))
+        psum = ctx.enter_context(tc.psum_pool(name="psum", bufs=1))
+
+        def load_list(name, src):
+            t = keep.tile(list(src.shape), U16, name=name)
+            nc.sync.dma_start(t[:], src)
+            return t
+
+        over = ctx.enter_context(tc.tile_pool(name="over", bufs=1))
+        tab_s = over.tile([P, T], U8, name="tab_s", align_bytes=64, offset=0)
+        nc.vector.memset(tab_s[:].bitcast(I32), 0)
+        offs_t = load_list("offs_t", offs)
+        for q in range(4):
+            nc.scalar.dma_start(tab_s[32 * q : 32 * q + 4, :].bitcast(I32), tab_scales[0, 4 * q : 4 * q + 4, :].bitcast(I32))
+        pos4_t = load_list("pos4_t", pos4)
+        pos2_t = load_list("pos2_t", pos2)
+        pos1_t = load_list("pos1_t", pos1)
+        w1_first = keep.tile([P, 4, 512], F32, name="w1_first", tag="raw8k")
+        nc.sync.dma_start(w1_first[:], w1[:, 0:512].rearrange("(p j) c -> p j c", j=4))
+        tab_w = keep.tile([P, T], I32, name="tab_w", tag="raw16k")
+        nc.sync.dma_start(tab_w[:], tab_words[0].rearrange("p t i -> p (t i)").bitcast(I32))
+        pos3_t = load_list("pos3_t", pos3)
+        gain_t = keep.tile([P, 2, 4], F32, name="gain_t")
+        nc.gpsimd.dma_start(gain_t[:], gain.rearrange("(a p t) -> p a t", a=2, t=4))
+        gain2_t = keep.tile([P, 4], F32, name="gain2_t")
+        gain2_rows = gain2.rearrange("(q t e) -> e q t", t=4, e=4)
+        with nc.allow_non_contiguous_dma(reason="one gain for each partition and word byte"):
+            for e in range(4):
+                nc.gpsimd.dma_start(gain2_t[e:P:4, :], gain2_rows[e])
+
+        v_s = keep.tile([P, S], U8, name="v_s", align_bytes=64)
+        nc.vector.tensor_copy(v_s[:], tab_s[:].indirect(offs_t[:]))
+        v_w = []
+        for c in range(S // BANK):
+            t = keep.tile([P, BANK], U32, name="v_w%d" % c, align_bytes=64)
+            nc.vector.tensor_copy(t[:], tab_w[:].bitcast(U32).indirect(offs_t[:, 32 * c : 32 * (c + 1)]))
+            v_w.append(t)
+
+        def quantise_weight(name, raw, s0, s1):
+            ns = s1 - s0
+            grouped = keep.tile([P, ns, P, 4], BF16, name=name + "_bf", align_bytes=64)
+            nc.scalar.copy(
+                grouped[:].rearrange("p s m j -> p m j s"),
+                raw.rearrange("p j (m s) -> p m j s", s=4)[:, :, :, s0:s1],
+            )
+            codes = keep.tile([P, ns * P], U32, name=name + "_c", align_bytes=64)
+            scales = keep.tile([P, ns * P], U8, name=name + "_s", align_bytes=64)
+            nc.vector.quantize_mx(codes[:].bitcast(FP8X4), scales[:], grouped[:].rearrange("p s m j -> p (s m j)"))
+            return [(codes[:, i * P : (i + 1) * P].bitcast(FP8X4), scales[:, i * P : (i + 1) * P]) for i in range(ns)]
+
+        w1_q = quantise_weight("w1a", w1_first[:], 0, 1) + quantise_weight("w1b", w1_first[:], 1, 4)
+
+        w1_second = keep.tile([P, 4, 512], F32, name="w1_second", tag="raw8k")
+        nc.sync.dma_start(w1_second[:], w1[:, 512:1024].rearrange("(p j) c -> p j c", j=4))
+        w2_raw = over.tile([P, 2, M // 2], I32, name="w2_raw", align_bytes=64, offset=0)
+        nc.sync.dma_start(w2_raw[:], w2_words.rearrange("a p c -> p a c").bitcast(I32))
+        w4s_raw = over.tile([P, N], U8, name="w4s_raw", align_bytes=64, offset=2048)
+        nc.gpsimd.memset(w4s_raw[:].bitcast(I32), 0)
+        w2s_raw = over.tile([P, 2 * M], U8, name="w2s_raw", align_bytes=64, offset=3072)
+        nc.gpsimd.memset(w2s_raw[:].bitcast(I32), 0)
+        for q in range(4):
+            nc.sync.dma_start(
+                w4s_raw[32 * q : 32 * q + 8, :].bitcast(I32), w4_scales[:, 4 * q : 4 * q + 4, :].bitcast(I32)
+            )
+        for q in range(4):
+            nc.sync.dma_start(
+                w2s_raw[32 * q : 32 * q + 4, :].bitcast(I32).rearrange("r (a c) -> r a c", a=2),
+                w2_scales[:, 4 * q : 4 * q + 4, :].bitcast(I32).rearrange("a r c -> r a c"),
+            )
+        w3_raw = keep.tile([P, 4, N], F32, name="w3_raw", tag="raw16k")
+        w3_rows = w3.rearrange("(q t e) n -> e q t n", t=4, e=4)
+        for e in range(4):
+            nc.sync.dma_start(w3_raw[e:P:4, :, :], w3_rows[e])
+
+        a1 = []
+        ref = []
+
+        def first_stage(s):
+            a, t = divmod(s, 4)
+            h = ring.tile([P, S], F32, name="h", bufs=3)
+            for c in range(S // BANK):
+                acc = psum.tile([P, BANK], F32, name="acc", bufs=4)
+                nc.tensor.matmul_mx(
+                    acc[:], lhsT=w1_q[s][0], lhsT_scale=w1_q[s][1],
+                    rhs=v_w[c][:].bitcast(FP8X4), rhs_scale=v_s[:, c * BANK : (c + 1) * BANK], start=True, stop=True,
+                )
+                nc.scalar.activation(h[:, c * BANK : (c + 1) * BANK], acc[:], ACT.Tanh)
+            g4 = ring.tile([P, KEPT], F32, name="g4")
+            nc.vector.tensor_copy(g4[:], h[:].indirect(pos4_t[:]))
+            r = keep.tile([P, KEPT], F32, name="ref%d" % s)
+            nc.scalar.activation(r[:], g4[:], ACT.Copy, scale=gain_t[:, a, t : t + 1])
+            ref.append(r)
+            g2 = ring.tile([P, PAIRS], F32, name="g2")
+            nc.vector.tensor_copy(g2[:], h[:].indirect(pos2_t[:]))
+            d = keep.tile([P, PAIRS], F32, name="a1_%d" % s)
+            nc.vector.tensor_tensor(d[:], h[:].indirect(pos1_t[:]), g2[:], ALU.subtract)
+            a1.append(d)
+
+        first_stage(0)
+        w1_q += quantise_weight("w1c", w1_second[:], 0, 4)
+        w4_raw = keep.tile([P, 2, N], I32, name="w4_raw", tag="raw8k")
+        nc.sync.dma_start(w4_raw[:], w4_words.rearrange("a p c i -> p a (c i)").bitcast(I32))
+        first_stage(1)
+
+        w4_c = keep.tile([P, 2 * N], I32, name="w4_c", align_bytes=64)
+        nc.vector.tensor_copy(
+            w4_c[:].rearrange("p (b s m) -> p b m s", s=4, m=P),
+            w4_raw[:].rearrange("p a (g m s) -> p (a g) m s", s=4, m=P),
+        )
+        w4_s = keep.tile([P, N], U8, name="w4_s", align_bytes=64)
+        nc.vector.tensor_copy(
+            w4_s[:].rearrange("p (g s m) -> p g m s", s=4, m=P),
+            w4s_raw[:].rearrange("p (g m s) -> p g m s", s=4, m=P),
+        )
+        w2_c = keep.tile([P, 2 * 2 * M], U8, name="w2_c", align_bytes=64)
+        nc.vector.tensor_copy(
+            w2_c[:].bitcast(I32).rearrange("p (a t q e) -> p a t q e", a=2, t=4, e=2),
+            w2_raw[:].rearrange("p a (q t e) -> p a t q e", t=4, e=2),
+        )
+        w2_s = keep.tile([P, 2 * M], U8, name="w2_s", align_bytes=64)
+        nc.vector.tensor_copy(
+            w2_s[:].bitcast(I32).rearrange("p (a t q) -> p a t q", a=2, t=4),
+            w2s_raw[:].bitcast(I32).rearrange("p (a q t) -> p a t q", a=2, t=4),
+        )
+        first_stage(2)
+        w3_q = quantise_weight("w3a", w3_raw[:, :, 0:512], 0, 4)
+        first_stage(3)
+        w3_q += quantise_weight("w3b", w3_raw[:, :, 512:1024], 0, 4)
+
+        y_scales = keep.tile([P, 2, KEPT], U8, name="y_scales", align_bytes=64)
+        out_rows = out_0.rearrange("(g p t) j -> g p t j", g=2, t=4)
+        out_words = out_1.rearrange("g p m t -> p g (m t)").bitcast(I32)
+
+        pick_buf = [keep.tile([P, 4 * UNIT], F32, name="pick_buf%d" % a, align_bytes=64) for a in range(2)]
+        tanh_buf = keep.tile([P, 4 * UNIT], F32, name="tanh_buf", align_bytes=64)
+        round_buf = keep.tile([P, 4 * UNIT], BF16, name="round_buf", align_bytes=64)
+        d_acc, y_acc = {}, {}
+
+        def bound_pairs(k):
+            u, a = divmod(k, 2)
+            x = pick_buf[a][:].rearrange("p (t c) -> p t c", t=4)
+            for t in range(4):
+                nc.vector.tensor_copy(x[:, t, :], a1[4 * a + t][:].indirect(pos3_t[:, 8 * u : 8 * (u + 1)]))
+            flat = round_buf[:] if a else tanh_buf[:].bitcast(BF16)[:, 0 : 4 * UNIT]
+            a2 = flat.rearrange("p (t c) -> p t c", t=4)
+            for t in range(4):
+                nc.vector.scalar_tensor_tensor(
+                    a2[:, t, :], x[:, t, :], gain_t[:, a, t : t + 1], ref[4 * a + t][:, u * UNIT : (u + 1) * UNIT],
+                    ALU.mult, ALU.min,
+                )
+            nc.scalar.copy(
+                pick_buf[a][:].bitcast(BF16)[:, 0 : 4 * UNIT].rearrange("p (c i t) -> p c t i", i=4, t=4),
+                a2.rearrange("p t (c i) -> p c t i", i=4),
+            )
+
+        def multiply_pairs(k):
+            u, a = divmod(k, 2)
+            if a == 0:
+                d_acc[u] = psum.tile([P, 4, UNIT], F32, name="acc", bufs=4)
+                y_acc[u] = [psum.tile([P, 4, UNIT], F32, name="y_acc%d" % g, bufs=2) for g in range(2)]
+            qa_c = ring.tile([P, UNIT], U32, name="qa_c", align_bytes=64)
+            qa_s = ring.tile([P, UNIT], U8, name="qa_s", align_bytes=64)
+            nc.vector.quantize_mx(qa_c[:].bitcast(FP8X4), qa_s[:], pick_buf[a][:].bitcast(BF16)[:, 0 : 4 * UNIT])
+            for t in range(4):
+                nc.tensor.matmul_mx(
+                    d_acc[u][:, t, :],
+                    lhsT=w2_c[:, (4 * a + t) * 256 : (4 * a + t + 1) * 256].bitcast(FP4X4),
+                    lhsT_scale=w2_s[:, (4 * a + t) * P : (4 * a + t + 1) * P],
+                    rhs=qa_c[:].bitcast(FP8X4), rhs_scale=qa_s[:],
+                    start=(a == 0 and t == 0), stop=(a == 1 and t == 3),
+                )
+            if a == 1:
+                nc.scalar.activation(
+                    tanh_buf[:].rearrange("p (c t) -> p c t", t=4), d_acc[u][:].rearrange("p t c -> p c t"), ACT.Tanh
+                )
+            for g in range(2):
+                for t in range(4):
+                    c0 = (4 * g + t) * P
+                    nc.tensor.matmul_mx(
+                        y_acc[u][g][:, t, :],
+                        lhsT=w4_c[:, a * N + c0 : a * N + c0 + P].bitcast(FP8X4),
+                        lhsT_scale=w4_s[4 * a : P, c0 : c0 + P],
+                        rhs=qa_c[:].bitcast(FP8X4), rhs_scale=qa_s[:],
+                        start=(a == 0 and t == 0), stop=False,
+                    )
+
+        def second_stage(u):
+            d_i = ring.tile([P, UNIT, 4], BF16, name="d_i", align_bytes=64)
+            nc.vector.tensor_tensor(
+                d_i[:], tanh_buf[:].rearrange("p (c t) -> p c t", t=4),
+                gain2_t[:].unsqueeze(1).to_broadcast([P, UNIT, 4]), ALU.mult,
+            )
+            qd_c = ring.tile([P, UNIT], U32, name="qd_c", align_bytes=64)
+            qd_s = ring.tile([P, UNIT], U8, name="qd_s", align_bytes=64)
+            nc.vector.quantize_mx(qd_c[:].bitcast(FP8X4), qd_s[:], d_i[:].rearrange("p c t -> p (c t)"))
+            for g in range(2):
+                for t in range(4):
+                    nc.tensor.matmul_mx(
+                        y_acc[u][g][:, t, :], lhsT=w3_q[4 * g + t][0], lhsT_scale=w3_q[4 * g + t][1],
+                        rhs=qd_c[:].bitcast(FP8X4), rhs_scale=qd_s[:], start=False, stop=(t == 3),
+                    )
+
+        def hand_out(u):
+            cols = slice(u * UNIT, (u + 1) * UNIT)
+            y_codes = ring.tile([P, 2, UNIT], I32, name="y_codes", align_bytes=64)
+            y_first = ring.tile([P, 4 * UNIT], BF16, name="y_first", align_bytes=64)
+            y_i = [y_first, round_buf]
+
+            def round_y(g):
+                dst = y_i[g][:].rearrange("p (c t) -> p c t", t=4)
+                if u == UNITS - 1:
+                    nc.vector.tensor_copy(dst, y_acc[u][g][:].rearrange("p t c -> p c t"))
+                else:
+                    nc.scalar.copy(dst, y_acc[u][g][:].rearrange("p t c -> p c t"))
+                nc.vector.quantize_mx(y_codes[:, g, :].bitcast(FP8X4), y_scales[:, g, cols], y_i[g][:])
+
+            def store_y(g):
+                y_f = ring.tile([P, 4, UNIT], F32, name="y_f%d" % g)
+                nc.scalar.copy(y_f[:], y_acc[u][g][:])
+                nc.sync.dma_start(out_rows[g][:, :, cols], y_f[:])
+
+            if u == UNITS - 1:
+                round_y(0)
+                store_y(1)
+                store_y(0)
+                round_y(1)
+            else:
+                round_y(0)
+                round_y(1)
+                store_y(0)
+                store_y(1)
+            nc.sync.dma_start(out_words[:, :, cols], y_codes[:])
+
+        first_stage(4)
+        bound_pairs(0)
+        first_stage(5)
+        multiply_pairs(0)
+        first_stage(6)
+        first_stage(7)
+        bound_pairs(1)
+        for k in range(2, 2 * UNITS):
+            bound_pairs(k)
+            multiply_pairs(k - 1)
+            if k % 2:
+                second_stage((k - 3) // 2)
+            elif k >= 4:
+                hand_out((k - 4) // 2)
+        multiply_pairs(2 * UNITS - 1)
+        second_stage(UNITS - 1)
+        hand_out(UNITS - 2)
+        hand_out(UNITS - 1)
+
+        for q in range(4):
+            eng = nc.scalar if q % 2 else nc.sync
+            eng.dma_start(
+                out_2[:, 4 * q : 4 * q + 4, :].bitcast(I32).rearrange("g r c -> r g c"),
+                y_scales[32 * q : 32 * q + 4, :, :].bitcast(I32),
+            )

@@ -39,18 +39,21 @@ def tile_list_spatter_pair_features_kernel(
 
         over = ctx.enter_context(tc.tile_pool(name="over", bufs=1))
         tab_s = over.tile([P, T], U8, name="tab_s", align_bytes=64, offset=0)
-        nc.vector.memset(tab_s[:].bitcast(I32), 0)
+        nc.sync.dma_start(tab_s[112:128, :].bitcast(I32), tab_scales[0].bitcast(I32))
         offs_t = load_list("offs_t", offs)
-        for q in range(4):
-            nc.scalar.dma_start(tab_s[32 * q : 32 * q + 4, :].bitcast(I32), tab_scales[0, 4 * q : 4 * q + 4, :].bitcast(I32))
-        pos4_t = load_list("pos4_t", pos4)
-        pos2_t = load_list("pos2_t", pos2)
-        pos1_t = load_list("pos1_t", pos1)
+        nc.vector.memset(tab_s[0:96, :].bitcast(I32), 0)
+        nc.vector.memset(tab_s[96:112, :].bitcast(I32), 0)
+        v_s = keep.tile([P, S], U8, name="v_s", align_bytes=64)
+        nc.gpsimd.memset(v_s[:].bitcast(I32), 0)
         w1_first = keep.tile([P, 4, 512], F32, name="w1_first", tag="raw8k")
         nc.sync.dma_start(w1_first[:], w1[:, 0:512].rearrange("(p j) c -> p j c", j=4))
         tab_w = keep.tile([P, T], I32, name="tab_w", tag="raw16k")
         nc.sync.dma_start(tab_w[:], tab_words[0].rearrange("p t i -> p (t i)").bitcast(I32))
-        pos3_t = load_list("pos3_t", pos3)
+        pos2_t = load_list("pos2_t", pos2)
+        pos4_t = load_list("pos4_t", pos4)
+        pos1_t = load_list("pos1_t", pos1)
+        w4_raw = keep.tile([P, 2, N], I32, name="w4_raw")
+        nc.sync.dma_start(w4_raw[:], w4_words.rearrange("a p c i -> p a (c i)").bitcast(I32))
         gain_t = keep.tile([P, 2, 4], F32, name="gain_t")
         nc.gpsimd.dma_start(gain_t[:], gain.rearrange("(a p t) -> p a t", a=2, t=4))
         gain2_t = keep.tile([P, 4], F32, name="gain2_t")
@@ -59,8 +62,13 @@ def tile_list_spatter_pair_features_kernel(
             for e in range(4):
                 nc.gpsimd.dma_start(gain2_t[e:P:4, :], gain2_rows[e])
 
-        v_s = keep.tile([P, S], U8, name="v_s", align_bytes=64)
-        nc.vector.tensor_copy(v_s[:], tab_s[:].indirect(offs_t[:]))
+        picked_s = keep.tile([P, S], U8, name="picked_s", align_bytes=64)
+        nc.vector.tensor_copy(picked_s[:], tab_s[:].indirect(offs_t[:]))
+        for q in range(4):
+            nc.sync.dma_start(
+                v_s[32 * q : 32 * q + 4, :].bitcast(I32), picked_s[112 + 4 * q : 116 + 4 * q, :].bitcast(I32)
+            )
+        pos3_t = load_list("pos3_t", pos3)
         v_w = []
         for c in range(S // BANK):
             t = keep.tile([P, BANK], U32, name="v_w%d" % c, align_bytes=64)
@@ -103,11 +111,18 @@ def tile_list_spatter_pair_features_kernel(
         for e in range(4):
             nc.sync.dma_start(w3_raw[e:P:4, :, :], w3_rows[e])
 
-        a1 = []
-        ref = []
+        w4_c = keep.tile([P, 2 * N], I32, name="w4_c", align_bytes=64)
+        nc.vector.tensor_copy(
+            w4_c[:].rearrange("p (b s m) -> p b m s", s=4, m=P),
+            w4_raw[:].rearrange("p a (g m s) -> p (a g) m s", s=4, m=P),
+        )
 
-        def first_stage(s):
-            a, t = divmod(s, 4)
+        a1 = []
+        ref = [keep.tile([P, 4, KEPT], F32, name="ref%d" % a) for a in range(2)]
+
+        tanh_rows = {}
+
+        def first_product(s):
             h = ring.tile([P, S], F32, name="h", bufs=3)
             for c in range(S // BANK):
                 acc = psum.tile([P, BANK], F32, name="acc", bufs=4)
@@ -116,28 +131,30 @@ def tile_list_spatter_pair_features_kernel(
                     rhs=v_w[c][:].bitcast(FP8X4), rhs_scale=v_s[:, c * BANK : (c + 1) * BANK], start=True, stop=True,
                 )
                 nc.scalar.activation(h[:, c * BANK : (c + 1) * BANK], acc[:], ACT.Tanh)
-            g4 = ring.tile([P, KEPT], F32, name="g4")
-            nc.vector.tensor_copy(g4[:], h[:].indirect(pos4_t[:]))
-            r = keep.tile([P, KEPT], F32, name="ref%d" % s)
-            nc.scalar.activation(r[:], g4[:], ACT.Copy, scale=gain_t[:, a, t : t + 1])
-            ref.append(r)
+            tanh_rows[s] = h
+
+        def first_stage(s):
+            a, t = divmod(s, 4)
+            h = tanh_rows[s]
             g2 = ring.tile([P, PAIRS], F32, name="g2")
             nc.vector.tensor_copy(g2[:], h[:].indirect(pos2_t[:]))
+            g4 = ring.tile([P, KEPT], F32, name="g4")
+            nc.vector.tensor_copy(g4[:], h[:].indirect(pos4_t[:]))
+            diff = ring.tile([P, PAIRS], F32, name="diff")
+            nc.vector.tensor_tensor(diff[:], h[:].indirect(pos1_t[:]), g2[:], ALU.subtract)
+            if s + 2 < 8:
+                first_product(s + 2)
+            nc.scalar.activation(ref[a][:, t, :], g4[:], ACT.Copy, scale=gain_t[:, a, t : t + 1])
             d = keep.tile([P, PAIRS], F32, name="a1_%d" % s)
-            nc.vector.tensor_tensor(d[:], h[:].indirect(pos1_t[:]), g2[:], ALU.subtract)
+            nc.scalar.activation(d[:], diff[:], ACT.Copy, scale=gain_t[:, a, t : t + 1])
             a1.append(d)
 
+        first_product(0)
+        first_product(1)
         first_stage(0)
         w1_q += quantise_weight("w1c", w1_second[:], 0, 4)
-        w4_raw = keep.tile([P, 2, N], I32, name="w4_raw", tag="raw8k")
-        nc.sync.dma_start(w4_raw[:], w4_words.rearrange("a p c i -> p a (c i)").bitcast(I32))
         first_stage(1)
 
-        w4_c = keep.tile([P, 2 * N], I32, name="w4_c", align_bytes=64)
-        nc.vector.tensor_copy(
-            w4_c[:].rearrange("p (b s m) -> p b m s", s=4, m=P),
-            w4_raw[:].rearrange("p a (g m s) -> p (a g) m s", s=4, m=P),
-        )
         w4_s = keep.tile([P, N], U8, name="w4_s", align_bytes=64)
         nc.vector.tensor_copy(
             w4_s[:].rearrange("p (g s m) -> p g m s", s=4, m=P),
@@ -162,26 +179,22 @@ def tile_list_spatter_pair_features_kernel(
         out_rows = out_0.rearrange("(g p t) j -> g p t j", g=2, t=4)
         out_words = out_1.rearrange("g p m t -> p g (m t)").bitcast(I32)
 
-        pick_buf = [keep.tile([P, 4 * UNIT], F32, name="pick_buf%d" % a, align_bytes=64) for a in range(2)]
-        tanh_buf = keep.tile([P, 4 * UNIT], F32, name="tanh_buf", align_bytes=64)
-        round_buf = keep.tile([P, 4 * UNIT], BF16, name="round_buf", align_bytes=64)
-        d_acc, y_acc = {}, {}
+        pick_buf = keep.tile([P, 4 * UNIT], F32, name="pick_buf", align_bytes=64)
+        woven = pick_buf[:].bitcast(BF16)[:, 4 * UNIT : 8 * UNIT]
+        d_acc, y_acc, d_t = {}, {}, {}
 
         def bound_pairs(k):
             u, a = divmod(k, 2)
-            x = pick_buf[a][:].rearrange("p (t c) -> p t c", t=4)
             for t in range(4):
-                nc.vector.tensor_copy(x[:, t, :], a1[4 * a + t][:].indirect(pos3_t[:, 8 * u : 8 * (u + 1)]))
-            flat = round_buf[:] if a else tanh_buf[:].bitcast(BF16)[:, 0 : 4 * UNIT]
-            a2 = flat.rearrange("p (t c) -> p t c", t=4)
-            for t in range(4):
-                nc.vector.scalar_tensor_tensor(
-                    a2[:, t, :], x[:, t, :], gain_t[:, a, t : t + 1], ref[4 * a + t][:, u * UNIT : (u + 1) * UNIT],
-                    ALU.mult, ALU.min,
+                nc.vector.tensor_copy(
+                    pick_buf[:, t * UNIT : (t + 1) * UNIT], a1[4 * a + t][:].indirect(pos3_t[:, 8 * u : 8 * (u + 1)])
                 )
+            a2 = ring.tile([P, 4, UNIT], BF16, name="a2")
+            nc.vector.tensor_tensor(
+                a2[:], pick_buf[:].rearrange("p (t c) -> p t c", t=4), ref[a][:, :, u * UNIT : (u + 1) * UNIT], ALU.min
+            )
             nc.scalar.copy(
-                pick_buf[a][:].bitcast(BF16)[:, 0 : 4 * UNIT].rearrange("p (c i t) -> p c t i", i=4, t=4),
-                a2.rearrange("p t (c i) -> p c t i", i=4),
+                woven.rearrange("p (c i t) -> p c t i", i=4, t=4), a2[:].rearrange("p t (c i) -> p c t i", i=4)
             )
 
         def multiply_pairs(k):
@@ -191,7 +204,7 @@ def tile_list_spatter_pair_features_kernel(
                 y_acc[u] = [psum.tile([P, 4, UNIT], F32, name="y_acc%d" % g, bufs=2) for g in range(2)]
             qa_c = ring.tile([P, UNIT], U32, name="qa_c", align_bytes=64)
             qa_s = ring.tile([P, UNIT], U8, name="qa_s", align_bytes=64)
-            nc.vector.quantize_mx(qa_c[:].bitcast(FP8X4), qa_s[:], pick_buf[a][:].bitcast(BF16)[:, 0 : 4 * UNIT])
+            nc.vector.quantize_mx(qa_c[:].bitcast(FP8X4), qa_s[:], woven)
             for t in range(4):
                 nc.tensor.matmul_mx(
                     d_acc[u][:, t, :],
@@ -201,9 +214,8 @@ def tile_list_spatter_pair_features_kernel(
                     start=(a == 0 and t == 0), stop=(a == 1 and t == 3),
                 )
             if a == 1:
-                nc.scalar.activation(
-                    tanh_buf[:].rearrange("p (c t) -> p c t", t=4), d_acc[u][:].rearrange("p t c -> p c t"), ACT.Tanh
-                )
+                d_t[u] = ring.tile([P, UNIT, 4], F32, name="d_t")
+                nc.scalar.activation(d_t[u][:], d_acc[u][:].rearrange("p t c -> p c t"), ACT.Tanh)
             for g in range(2):
                 for t in range(4):
                     c0 = (4 * g + t) * P
@@ -218,7 +230,7 @@ def tile_list_spatter_pair_features_kernel(
         def second_stage(u):
             d_i = ring.tile([P, UNIT, 4], BF16, name="d_i", align_bytes=64)
             nc.vector.tensor_tensor(
-                d_i[:], tanh_buf[:].rearrange("p (c t) -> p c t", t=4),
+                d_i[:], d_t[u][:],
                 gain2_t[:].unsqueeze(1).to_broadcast([P, UNIT, 4]), ALU.mult,
             )
             qd_c = ring.tile([P, UNIT], U32, name="qd_c", align_bytes=64)
@@ -234,8 +246,7 @@ def tile_list_spatter_pair_features_kernel(
         def hand_out(u):
             cols = slice(u * UNIT, (u + 1) * UNIT)
             y_codes = ring.tile([P, 2, UNIT], I32, name="y_codes", align_bytes=64)
-            y_first = ring.tile([P, 4 * UNIT], BF16, name="y_first", align_bytes=64)
-            y_i = [y_first, round_buf]
+            y_i = [ring.tile([P, 4 * UNIT], BF16, name="y_i%d" % g, align_bytes=64) for g in range(2)]
 
             def round_y(g):
                 dst = y_i[g][:].rearrange("p (c t) -> p c t", t=4)
@@ -243,21 +254,26 @@ def tile_list_spatter_pair_features_kernel(
                     nc.vector.tensor_copy(dst, y_acc[u][g][:].rearrange("p t c -> p c t"))
                 else:
                     nc.scalar.copy(dst, y_acc[u][g][:].rearrange("p t c -> p c t"))
-                nc.vector.quantize_mx(y_codes[:, g, :].bitcast(FP8X4), y_scales[:, g, cols], y_i[g][:])
 
             def store_y(g):
                 y_f = ring.tile([P, 4, UNIT], F32, name="y_f%d" % g)
                 nc.scalar.copy(y_f[:], y_acc[u][g][:])
                 nc.sync.dma_start(out_rows[g][:, :, cols], y_f[:])
 
+            def quantise_y():
+                for g in range(2):
+                    nc.vector.quantize_mx(y_codes[:, g, :].bitcast(FP8X4), y_scales[:, g, cols], y_i[g][:])
+
             if u == UNITS - 1:
                 round_y(0)
                 store_y(1)
                 store_y(0)
                 round_y(1)
+                quantise_y()
             else:
                 round_y(0)
                 round_y(1)
+                quantise_y()
                 store_y(0)
                 store_y(1)
             nc.sync.dma_start(out_words[:, :, cols], y_codes[:])
@@ -268,17 +284,14 @@ def tile_list_spatter_pair_features_kernel(
         multiply_pairs(0)
         first_stage(6)
         first_stage(7)
-        bound_pairs(1)
-        for k in range(2, 2 * UNITS):
+        for k in range(1, 2 * UNITS):
             bound_pairs(k)
-            multiply_pairs(k - 1)
-            if k % 2:
-                second_stage((k - 3) // 2)
-            elif k >= 4:
-                hand_out((k - 4) // 2)
-        multiply_pairs(2 * UNITS - 1)
+            if k % 2 == 0:
+                second_stage(k // 2 - 1)
+            elif k >= 3:
+                hand_out(k // 2 - 1)
+            multiply_pairs(k)
         second_stage(UNITS - 1)
-        hand_out(UNITS - 2)
         hand_out(UNITS - 1)
 
         for q in range(4):

@@ -42,7 +42,7 @@ def tile_list_spatter_pair_features_kernel(
         nc.sync.dma_start(tab_s[112:128, :].bitcast(I32), tab_scales[0].bitcast(I32))
         offs_t = load_list("offs_t", offs)
         nc.vector.memset(tab_s[0:96, :].bitcast(I32), 0)
-        nc.vector.memset(tab_s[96:112, :].bitcast(I32), 0)
+        nc.gpsimd.memset(tab_s[96:112, :].bitcast(I32), 0)
         v_s = keep.tile([P, S], U8, name="v_s", align_bytes=64)
         nc.gpsimd.memset(v_s[:].bitcast(I32), 0)
         w1_first = keep.tile([P, 4, 512], F32, name="w1_first", tag="raw8k")
@@ -52,51 +52,46 @@ def tile_list_spatter_pair_features_kernel(
         pos2_t = load_list("pos2_t", pos2)
         pos4_t = load_list("pos4_t", pos4)
         pos1_t = load_list("pos1_t", pos1)
-        w4_raw = keep.tile([P, 2, N], I32, name="w4_raw")
-        nc.sync.dma_start(w4_raw[:], w4_words.rearrange("a p c i -> p a (c i)").bitcast(I32))
-        gain_t = keep.tile([P, 2, 4], F32, name="gain_t")
-        nc.gpsimd.dma_start(gain_t[:], gain.rearrange("(a p t) -> p a t", a=2, t=4))
-        gain2_t = keep.tile([P, 4], F32, name="gain2_t")
-        gain2_rows = gain2.rearrange("(q t e) -> e q t", t=4, e=4)
-        with nc.allow_non_contiguous_dma(reason="one gain for each partition and word byte"):
-            for e in range(4):
-                nc.gpsimd.dma_start(gain2_t[e:P:4, :], gain2_rows[e])
+        pos3_t = load_list("pos3_t", pos3)
 
-        picked_s = keep.tile([P, S], U8, name="picked_s", align_bytes=64)
+        picked_s = over.tile([P, S], U8, name="picked_s", align_bytes=64, offset=12288)
         nc.vector.tensor_copy(picked_s[:], tab_s[:].indirect(offs_t[:]))
         for q in range(4):
             nc.sync.dma_start(
                 v_s[32 * q : 32 * q + 4, :].bitcast(I32), picked_s[112 + 4 * q : 116 + 4 * q, :].bitcast(I32)
             )
-        pos3_t = load_list("pos3_t", pos3)
-        v_w = []
-        for c in range(S // BANK):
-            t = keep.tile([P, BANK], U32, name="v_w%d" % c, align_bytes=64)
-            nc.vector.tensor_copy(t[:], tab_w[:].bitcast(U32).indirect(offs_t[:, 32 * c : 32 * (c + 1)]))
-            v_w.append(t)
+
+        w4_raw = over.tile([P, 2, N], I32, name="w4_raw", align_bytes=64, offset=4032)
+        nc.sync.dma_start(w4_raw[:], w4_words.rearrange("a p c i -> p a (c i)").bitcast(I32))
+        gain_t = over.tile([P, 2, 4], F32, name="gain_t", align_bytes=64, offset=2048)
+        nc.sync.dma_start(gain_t[:], gain.rearrange("(a p t) -> p a t", a=2, t=4))
+        w4s_raw = over.tile([P, N], U8, name="w4s_raw", align_bytes=64, offset=0)
+        nc.vector.memset(w4s_raw[:].bitcast(I32), 0)
+        w2s_raw = over.tile([P, 2 * M], U8, name="w2s_raw", align_bytes=64, offset=1024)
+        nc.vector.memset(w2s_raw[:].bitcast(I32), 0)
 
         def quantise_weight(name, raw, s0, s1):
             ns = s1 - s0
             grouped = keep.tile([P, ns, P, 4], BF16, name=name + "_bf", align_bytes=64)
             nc.scalar.copy(
-                grouped[:].rearrange("p s m j -> p m j s"),
-                raw.rearrange("p j (m s) -> p m j s", s=4)[:, :, :, s0:s1],
+                grouped[:].rearrange("p (r i) m j -> p r m j i", i=2),
+                raw.rearrange("p j (m r i) -> p r m j i", r=2, i=2)[:, s0 // 2 : s1 // 2],
             )
             codes = keep.tile([P, ns * P], U32, name=name + "_c", align_bytes=64)
             scales = keep.tile([P, ns * P], U8, name=name + "_s", align_bytes=64)
             nc.vector.quantize_mx(codes[:].bitcast(FP8X4), scales[:], grouped[:].rearrange("p s m j -> p (s m j)"))
             return [(codes[:, i * P : (i + 1) * P].bitcast(FP8X4), scales[:, i * P : (i + 1) * P]) for i in range(ns)]
 
-        w1_q = quantise_weight("w1a", w1_first[:], 0, 1) + quantise_weight("w1b", w1_first[:], 1, 4)
+        w1_q = quantise_weight("w1a", w1_first[:], 0, 2) + quantise_weight("w1b", w1_first[:], 2, 4)
+
+        v_w = []
+        for c in range(S // BANK):
+            t = keep.tile([P, BANK], U32, name="v_w%d" % c, align_bytes=64)
+            nc.vector.tensor_copy(t[:], tab_w[:].bitcast(U32).indirect(offs_t[:, 32 * c : 32 * (c + 1)]))
+            v_w.append(t)
 
         w1_second = keep.tile([P, 4, 512], F32, name="w1_second", tag="raw8k")
         nc.sync.dma_start(w1_second[:], w1[:, 512:1024].rearrange("(p j) c -> p j c", j=4))
-        w2_raw = over.tile([P, 2, M // 2], I32, name="w2_raw", align_bytes=64, offset=0)
-        nc.sync.dma_start(w2_raw[:], w2_words.rearrange("a p c -> p a c").bitcast(I32))
-        w4s_raw = over.tile([P, N], U8, name="w4s_raw", align_bytes=64, offset=2048)
-        nc.gpsimd.memset(w4s_raw[:].bitcast(I32), 0)
-        w2s_raw = over.tile([P, 2 * M], U8, name="w2s_raw", align_bytes=64, offset=3072)
-        nc.gpsimd.memset(w2s_raw[:].bitcast(I32), 0)
         for q in range(4):
             nc.sync.dma_start(
                 w4s_raw[32 * q : 32 * q + 8, :].bitcast(I32), w4_scales[:, 4 * q : 4 * q + 4, :].bitcast(I32)
@@ -106,15 +101,22 @@ def tile_list_spatter_pair_features_kernel(
                 w2s_raw[32 * q : 32 * q + 4, :].bitcast(I32).rearrange("r (a c) -> r a c", a=2),
                 w2_scales[:, 4 * q : 4 * q + 4, :].bitcast(I32).rearrange("a r c -> r a c"),
             )
+        w2_raw = over.tile([P, 2, M // 2], I32, name="w2_raw", align_bytes=64, offset=12288)
+        nc.sync.dma_start(w2_raw[:], w2_words.rearrange("a p c -> p a c").bitcast(I32))
         w3_raw = keep.tile([P, 4, N], F32, name="w3_raw", tag="raw16k")
         w3_rows = w3.rearrange("(q t e) n -> e q t n", t=4, e=4)
         for e in range(4):
             nc.sync.dma_start(w3_raw[e:P:4, :, :], w3_rows[e])
+        gain2_t = over.tile([P, 4], F32, name="gain2_t", align_bytes=64, offset=2112)
+        gain2_rows = gain2.rearrange("(q t e) -> e q t", t=4, e=4)
+        with nc.allow_non_contiguous_dma(reason="one gain for each partition and word byte"):
+            for e in range(4):
+                nc.sync.dma_start(gain2_t[e:P:4, :], gain2_rows[e])
 
         w4_c = keep.tile([P, 2 * N], I32, name="w4_c", align_bytes=64)
         nc.vector.tensor_copy(
-            w4_c[:].rearrange("p (b s m) -> p b m s", s=4, m=P),
-            w4_raw[:].rearrange("p a (g m s) -> p (a g) m s", s=4, m=P),
+            w4_c[:].rearrange("p (b s m i) -> p b m s i", s=4, m=P // 4, i=4),
+            w4_raw[:].rearrange("p a (g m i s) -> p (a g) m s i", s=4, m=P // 4, i=4),
         )
 
         a1 = []
@@ -157,8 +159,8 @@ def tile_list_spatter_pair_features_kernel(
 
         w4_s = keep.tile([P, N], U8, name="w4_s", align_bytes=64)
         nc.vector.tensor_copy(
-            w4_s[:].rearrange("p (g s m) -> p g m s", s=4, m=P),
-            w4s_raw[:].rearrange("p (g m s) -> p g m s", s=4, m=P),
+            w4_s[:].rearrange("p (g s m) -> p g s m", s=4, m=P),
+            w4s_raw[:].rearrange("p (g m s) -> p g s m", s=4, m=P),
         )
         w2_c = keep.tile([P, 2 * 2 * M], U8, name="w2_c", align_bytes=64)
         nc.vector.tensor_copy(
@@ -179,38 +181,40 @@ def tile_list_spatter_pair_features_kernel(
         out_rows = out_0.rearrange("(g p t) j -> g p t j", g=2, t=4)
         out_words = out_1.rearrange("g p m t -> p g (m t)").bitcast(I32)
 
-        pick_buf = keep.tile([P, 4 * UNIT], F32, name="pick_buf", align_bytes=64)
-        woven = pick_buf[:].bitcast(BF16)[:, 4 * UNIT : 8 * UNIT]
         d_acc, y_acc, d_t = {}, {}, {}
 
-        def bound_pairs(k):
-            u, a = divmod(k, 2)
+        def bound_pairs(a, c0, width, buf):
             for t in range(4):
                 nc.vector.tensor_copy(
-                    pick_buf[:, t * UNIT : (t + 1) * UNIT], a1[4 * a + t][:].indirect(pos3_t[:, 8 * u : 8 * (u + 1)])
+                    buf[:, t * width : (t + 1) * width],
+                    a1[4 * a + t][:].indirect(pos3_t[:, c0 // 16 : (c0 + width) // 16]),
                 )
-            a2 = ring.tile([P, 4, UNIT], BF16, name="a2")
+            a2 = ring.tile([P, 4, width], BF16, name="a2_%d" % a, bufs=1 + a)
             nc.vector.tensor_tensor(
-                a2[:], pick_buf[:].rearrange("p (t c) -> p t c", t=4), ref[a][:, :, u * UNIT : (u + 1) * UNIT], ALU.min
+                a2[:], buf[:, 0 : 4 * width].rearrange("p (t c) -> p t c", t=4), ref[a][:, :, c0 : c0 + width], ALU.min
             )
+            woven = buf[:].bitcast(BF16)[:, 6 * width : 10 * width]
             nc.scalar.copy(
                 woven.rearrange("p (c i t) -> p c t i", i=4, t=4), a2[:].rearrange("p t (c i) -> p c t i", i=4)
             )
+            return woven
 
-        def multiply_pairs(k):
-            u, a = divmod(k, 2)
+        def quantise_pairs(a, width, woven):
+            codes = ring.tile([P, width], U32, name="qa_c%d" % a, align_bytes=64, bufs=1 + a)
+            scales = ring.tile([P, width], U8, name="qa_s%d" % a, align_bytes=64, bufs=1 + a)
+            nc.vector.quantize_mx(codes[:].bitcast(FP8X4), scales[:], woven)
+            return codes, scales
+
+        def multiply_pairs(u, a, codes, scales):
             if a == 0:
                 d_acc[u] = psum.tile([P, 4, UNIT], F32, name="acc", bufs=4)
                 y_acc[u] = [psum.tile([P, 4, UNIT], F32, name="y_acc%d" % g, bufs=2) for g in range(2)]
-            qa_c = ring.tile([P, UNIT], U32, name="qa_c", align_bytes=64)
-            qa_s = ring.tile([P, UNIT], U8, name="qa_s", align_bytes=64)
-            nc.vector.quantize_mx(qa_c[:].bitcast(FP8X4), qa_s[:], woven)
             for t in range(4):
                 nc.tensor.matmul_mx(
                     d_acc[u][:, t, :],
                     lhsT=w2_c[:, (4 * a + t) * 256 : (4 * a + t + 1) * 256].bitcast(FP4X4),
                     lhsT_scale=w2_s[:, (4 * a + t) * P : (4 * a + t + 1) * P],
-                    rhs=qa_c[:].bitcast(FP8X4), rhs_scale=qa_s[:],
+                    rhs=codes.bitcast(FP8X4), rhs_scale=scales,
                     start=(a == 0 and t == 0), stop=(a == 1 and t == 3),
                 )
             if a == 1:
@@ -223,7 +227,7 @@ def tile_list_spatter_pair_features_kernel(
                         y_acc[u][g][:, t, :],
                         lhsT=w4_c[:, a * N + c0 : a * N + c0 + P].bitcast(FP8X4),
                         lhsT_scale=w4_s[4 * a : P, c0 : c0 + P],
-                        rhs=qa_c[:].bitcast(FP8X4), rhs_scale=qa_s[:],
+                        rhs=codes.bitcast(FP8X4), rhs_scale=scales,
                         start=(a == 0 and t == 0), stop=False,
                     )
 
@@ -279,19 +283,25 @@ def tile_list_spatter_pair_features_kernel(
             nc.sync.dma_start(out_words[:, :, cols], y_codes[:])
 
         first_stage(4)
-        bound_pairs(0)
+        wide_buf = keep.tile([P, 5 * KEPT], F32, name="wide_buf", align_bytes=64)
+        wide = bound_pairs(0, 0, KEPT, wide_buf)
         first_stage(5)
-        multiply_pairs(0)
+        low_c, low_s = quantise_pairs(0, KEPT, wide)
         first_stage(6)
         first_stage(7)
-        for k in range(1, 2 * UNITS):
-            bound_pairs(k)
-            if k % 2 == 0:
-                second_stage(k // 2 - 1)
-            elif k >= 3:
-                hand_out(k // 2 - 1)
-            multiply_pairs(k)
+        unit_buf = keep.tile([P, 5 * UNIT], F32, name="unit_buf", align_bytes=64)
+        for u in range(UNITS):
+            cols = slice(u * UNIT, (u + 1) * UNIT)
+            woven = bound_pairs(1, u * UNIT, UNIT, unit_buf)
+            if u >= 1:
+                second_stage(u - 1)
+            if u >= 2:
+                hand_out(u - 2)
+            multiply_pairs(u, 0, low_c[:, cols], low_s[:, cols])
+            high_c, high_s = quantise_pairs(1, UNIT, woven)
+            multiply_pairs(u, 1, high_c[:], high_s[:])
         second_stage(UNITS - 1)
+        hand_out(UNITS - 2)
         hand_out(UNITS - 1)
 
         for q in range(4):

@@ -127,7 +127,7 @@ def tile_list_spatter_pair_features_kernel(
         def first_product(s):
             h = ring.tile([P, S], F32, name="h", bufs=3)
             for c in range(S // BANK):
-                acc = psum.tile([P, BANK], F32, name="acc", bufs=4)
+                acc = psum.tile([P, BANK], F32, name="h_acc%d" % c, offset=2048 * c)
                 nc.tensor.matmul_mx(
                     acc[:], lhsT=w1_q[s][0], lhsT_scale=w1_q[s][1],
                     rhs=v_w[c][:].bitcast(FP8X4), rhs_scale=v_s[:, c * BANK : (c + 1) * BANK], start=True, stop=True,
@@ -189,15 +189,19 @@ def tile_list_spatter_pair_features_kernel(
                     buf[:, t * width : (t + 1) * width],
                     a1[4 * a + t][:].indirect(pos3_t[:, c0 // 16 : (c0 + width) // 16]),
                 )
-            a2 = ring.tile([P, 4, width], BF16, name="a2_%d" % a, bufs=1 + a)
-            nc.vector.tensor_tensor(
-                a2[:], buf[:, 0 : 4 * width].rearrange("p (t c) -> p t c", t=4), ref[a][:, :, c0 : c0 + width], ALU.min
-            )
-            woven = buf[:].bitcast(BF16)[:, 6 * width : 10 * width]
-            nc.scalar.copy(
-                woven.rearrange("p (c i t) -> p c t i", i=4, t=4), a2[:].rearrange("p t (c i) -> p c t i", i=4)
-            )
-            return woven
+            picked = buf[:].rearrange("p (t c i) -> p c t i", t=4, i=4)
+            bound = ref[a][:, :, c0 : c0 + width].rearrange("p t (c i) -> p c t i", i=4)
+            woven = ring.tile([P, 4 * width], BF16, name="woven%d" % a, align_bytes=64, bufs=1 + a)
+            dst = woven[:].rearrange("p (c i t) -> p c t i", i=4, t=4)
+            if a == 1:
+                nc.vector.tensor_tensor(dst, picked, bound, ALU.min)
+            else:
+                a2 = keep.tile([P, 4, width], BF16, name="a2")
+                nc.vector.tensor_tensor(
+                    a2[:], buf[:].rearrange("p (t c) -> p t c", t=4), ref[a][:, :, c0 : c0 + width], ALU.min
+                )
+                nc.scalar.copy(dst, a2[:].rearrange("p t (c i) -> p c t i", i=4))
+            return woven[:]
 
         def quantise_pairs(a, width, woven):
             codes = ring.tile([P, width], U32, name="qa_c%d" % a, align_bytes=64, bufs=1 + a)
@@ -207,8 +211,11 @@ def tile_list_spatter_pair_features_kernel(
 
         def multiply_pairs(u, a, codes, scales):
             if a == 0:
-                d_acc[u] = psum.tile([P, 4, UNIT], F32, name="acc", bufs=4)
-                y_acc[u] = [psum.tile([P, 4, UNIT], F32, name="y_acc%d" % g, bufs=2) for g in range(2)]
+                d_acc[u] = psum.tile([P, 4, UNIT], F32, name="d_acc%d" % u, offset=2048 * (u % 2))
+                y_acc[u] = [
+                    psum.tile([P, 4, UNIT], F32, name="y_acc%d_%d" % (u, g), offset=2048 * ((2 * u + 2) % 6 + 2 + g))
+                    for g in range(2)
+                ]
             for t in range(4):
                 nc.tensor.matmul_mx(
                     d_acc[u][:, t, :],
@@ -247,62 +254,55 @@ def tile_list_spatter_pair_features_kernel(
                         rhs=qd_c[:].bitcast(FP8X4), rhs_scale=qd_s[:], start=False, stop=(t == 3),
                     )
 
-        def hand_out(u):
-            cols = slice(u * UNIT, (u + 1) * UNIT)
-            y_codes = ring.tile([P, 2, UNIT], I32, name="y_codes", align_bytes=64)
-            y_i = [ring.tile([P, 4 * UNIT], BF16, name="y_i%d" % g, align_bytes=64) for g in range(2)]
+        y_i = {}
 
-            def round_y(g):
-                dst = y_i[g][:].rearrange("p (c t) -> p c t", t=4)
-                if u == UNITS - 1:
+        def empty_y(u):
+            for g in range(2):
+                y_i[u, g] = ring.tile([P, 4 * UNIT], BF16, name="y_i%d" % g, align_bytes=64)
+                dst = y_i[u, g][:].rearrange("p (c t) -> p c t", t=4)
+                if 2 * u + g >= 2 * UNITS - 3:
                     nc.vector.tensor_copy(dst, y_acc[u][g][:].rearrange("p t c -> p c t"))
                 else:
                     nc.scalar.copy(dst, y_acc[u][g][:].rearrange("p t c -> p c t"))
-
-            def store_y(g):
+            for g in range(2):
                 y_f = ring.tile([P, 4, UNIT], F32, name="y_f%d" % g)
-                nc.scalar.copy(y_f[:], y_acc[u][g][:])
-                nc.sync.dma_start(out_rows[g][:, :, cols], y_f[:])
+                if 2 * u + g == 2 * UNITS - 1:
+                    nc.vector.tensor_copy(y_f[:], y_acc[u][g][:])
+                else:
+                    nc.scalar.copy(y_f[:], y_acc[u][g][:])
+                nc.sync.dma_start(out_rows[g][:, :, u * UNIT : (u + 1) * UNIT], y_f[:])
 
-            def quantise_y():
-                for g in range(2):
-                    nc.vector.quantize_mx(y_codes[:, g, :].bitcast(FP8X4), y_scales[:, g, cols], y_i[g][:])
-
-            if u == UNITS - 1:
-                round_y(0)
-                store_y(1)
-                store_y(0)
-                round_y(1)
-                quantise_y()
-            else:
-                round_y(0)
-                round_y(1)
-                quantise_y()
-                store_y(0)
-                store_y(1)
+        def quantise_y(u):
+            cols = slice(u * UNIT, (u + 1) * UNIT)
+            y_codes = ring.tile([P, 2, UNIT], I32, name="y_codes", align_bytes=64)
+            for g in range(2):
+                nc.vector.quantize_mx(y_codes[:, g, :].bitcast(FP8X4), y_scales[:, g, cols], y_i[u, g][:])
             nc.sync.dma_start(out_words[:, :, cols], y_codes[:])
 
         first_stage(4)
-        wide_buf = keep.tile([P, 5 * KEPT], F32, name="wide_buf", align_bytes=64)
+        wide_buf = keep.tile([P, 4 * KEPT], F32, name="wide_buf", align_bytes=64)
         wide = bound_pairs(0, 0, KEPT, wide_buf)
         first_stage(5)
         low_c, low_s = quantise_pairs(0, KEPT, wide)
         first_stage(6)
         first_stage(7)
-        unit_buf = keep.tile([P, 5 * UNIT], F32, name="unit_buf", align_bytes=64)
+        unit_buf = keep.tile([P, 4 * UNIT], F32, name="unit_buf", align_bytes=64)
         for u in range(UNITS):
             cols = slice(u * UNIT, (u + 1) * UNIT)
+            multiply_pairs(u, 0, low_c[:, cols], low_s[:, cols])
             woven = bound_pairs(1, u * UNIT, UNIT, unit_buf)
+            high_c, high_s = quantise_pairs(1, UNIT, woven)
+            multiply_pairs(u, 1, high_c[:], high_s[:])
             if u >= 1:
                 second_stage(u - 1)
             if u >= 2:
-                hand_out(u - 2)
-            multiply_pairs(u, 0, low_c[:, cols], low_s[:, cols])
-            high_c, high_s = quantise_pairs(1, UNIT, woven)
-            multiply_pairs(u, 1, high_c[:], high_s[:])
+                empty_y(u - 2)
+                quantise_y(u - 2)
         second_stage(UNITS - 1)
-        hand_out(UNITS - 2)
-        hand_out(UNITS - 1)
+        for u in range(UNITS - 2, UNITS):
+            empty_y(u)
+        for u in range(UNITS - 2, UNITS):
+            quantise_y(u)
 
         for q in range(4):
             eng = nc.scalar if q % 2 else nc.sync

@@ -16,10 +16,25 @@ ALU = mybir.AluOpType
 T, S, PAIRS, KEPT = 4096, 2048, 1024, 512
 K, H, M, N = 512, 1024, 512, 1024
 P = 128
+PASS = 512
 BANK = 512
+BANK_BYTES = 4 * BANK
+SLICES = H // P
+AHEAD = 2
 UNIT = 128
 UNITS = KEPT // UNIT
+SCALE_ROW0 = P - 16
 FLOPS = 2 * (K * H * S + H * M * KEPT + M * N * KEPT + H * N * KEPT)
+
+AT_TAB_SCALES = 0
+AT_W4_SCALES_RAW = 0
+AT_W2_SCALES_RAW = 1024
+AT_GAIN = 2048
+AT_GAIN2 = 2112
+AT_W4_RAW = T - 64
+AT_PICKED_SCALES = 12288
+AT_TAB_WORDS = 14336
+AT_W1_ROUNDED = 30720
 
 
 def tile_list_spatter_pair_features_kernel(
@@ -30,49 +45,56 @@ def tile_list_spatter_pair_features_kernel(
     with ExitStack() as ctx:
         keep = ctx.enter_context(tc.tile_pool(name="keep", bufs=1))
         ring = ctx.enter_context(tc.tile_pool(name="ring", bufs=2))
+        placed = ctx.enter_context(tc.tile_pool(name="placed", bufs=1))
         psum = ctx.enter_context(tc.psum_pool(name="psum", bufs=1))
+
+        def place(name, shape, dtype, at):
+            return placed.tile(shape, dtype, name=name, align_bytes=64, offset=at)
 
         def load_list(name, src):
             t = keep.tile(list(src.shape), U16, name=name)
             nc.sync.dma_start(t[:], src)
             return t
 
-        over = ctx.enter_context(tc.tile_pool(name="over", bufs=1))
-        tab_s = over.tile([P, T], U8, name="tab_s", align_bytes=64, offset=0)
-        nc.sync.dma_start(tab_s[112:128, :].bitcast(I32), tab_scales[0].bitcast(I32))
+        tab_s = place("tab_s", [P, T], U8, AT_TAB_SCALES)
+        nc.sync.dma_start(tab_s[SCALE_ROW0:P, :].bitcast(I32), tab_scales[0].bitcast(I32))
         offs_t = load_list("offs_t", offs)
         nc.vector.memset(tab_s[0:96, :].bitcast(I32), 0)
-        nc.gpsimd.memset(tab_s[96:112, :].bitcast(I32), 0)
+        nc.gpsimd.memset(tab_s[96:SCALE_ROW0, :].bitcast(I32), 0)
         v_s = keep.tile([P, S], U8, name="v_s", align_bytes=64)
         nc.gpsimd.memset(v_s[:].bitcast(I32), 0)
-        w1_first = keep.tile([P, 4, 512], F32, name="w1_first", tag="raw8k")
-        nc.sync.dma_start(w1_first[:], w1[:, 0:512].rearrange("(p j) c -> p j c", j=4))
-        tab_w = keep.tile([P, T], I32, name="tab_w", tag="raw16k")
+        tab_w = place("tab_w", [P, T], I32, AT_TAB_WORDS)
         nc.sync.dma_start(tab_w[:], tab_words[0].rearrange("p t i -> p (t i)").bitcast(I32))
         pos2_t = load_list("pos2_t", pos2)
+        w1_first = keep.tile([P, 4, PASS], F32, name="w1_first", tag="w1_raw")
+        nc.sync.dma_start(w1_first[:], w1[:, 0:PASS].rearrange("(p j) c -> p j c", j=4))
         pos4_t = load_list("pos4_t", pos4)
         pos1_t = load_list("pos1_t", pos1)
         pos3_t = load_list("pos3_t", pos3)
 
-        picked_s = over.tile([P, S], U8, name="picked_s", align_bytes=64, offset=12288)
+        picked_s = place("picked_s", [P, S], U8, AT_PICKED_SCALES)
         nc.vector.tensor_copy(picked_s[:], tab_s[:].indirect(offs_t[:]))
         for q in range(4):
             nc.sync.dma_start(
-                v_s[32 * q : 32 * q + 4, :].bitcast(I32), picked_s[112 + 4 * q : 116 + 4 * q, :].bitcast(I32)
+                v_s[32 * q : 32 * q + 4, :].bitcast(I32),
+                picked_s[SCALE_ROW0 + 4 * q : SCALE_ROW0 + 4 * q + 4, :].bitcast(I32),
             )
 
-        w4_raw = over.tile([P, 2, N], I32, name="w4_raw", align_bytes=64, offset=4032)
+        w4_raw = place("w4_raw", [P, 2, N], I32, AT_W4_RAW)
         nc.sync.dma_start(w4_raw[:], w4_words.rearrange("a p c i -> p a (c i)").bitcast(I32))
-        gain_t = over.tile([P, 2, 4], F32, name="gain_t", align_bytes=64, offset=2048)
+        gain_t = place("gain_t", [P, 2, 4], F32, AT_GAIN)
         nc.sync.dma_start(gain_t[:], gain.rearrange("(a p t) -> p a t", a=2, t=4))
-        w4s_raw = over.tile([P, N], U8, name="w4s_raw", align_bytes=64, offset=0)
-        nc.vector.memset(w4s_raw[:].bitcast(I32), 0)
-        w2s_raw = over.tile([P, 2 * M], U8, name="w2s_raw", align_bytes=64, offset=1024)
-        nc.vector.memset(w2s_raw[:].bitcast(I32), 0)
+        w4s_raw = place("w4s_raw", [P, N], U8, AT_W4_SCALES_RAW)
+        nc.gpsimd.memset(w4s_raw[:].bitcast(I32), 0)
+        w2s_raw = place("w2s_raw", [P, 2 * M], U8, AT_W2_SCALES_RAW)
+        nc.gpsimd.memset(w2s_raw[:].bitcast(I32), 0)
 
-        def quantise_weight(name, raw, s0, s1):
+        def quantise_weight(name, raw, s0, s1, at=None):
             ns = s1 - s0
-            grouped = keep.tile([P, ns, P, 4], BF16, name=name + "_bf", align_bytes=64)
+            if at is None:
+                grouped = keep.tile([P, ns, P, 4], BF16, name=name + "_bf", align_bytes=64)
+            else:
+                grouped = place(name + "_bf", [P, ns, P, 4], BF16, at)
             nc.scalar.copy(
                 grouped[:].rearrange("p (r i) m j -> p r m j i", i=2),
                 raw.rearrange("p j (m r i) -> p r m j i", r=2, i=2)[:, s0 // 2 : s1 // 2],
@@ -82,16 +104,20 @@ def tile_list_spatter_pair_features_kernel(
             nc.vector.quantize_mx(codes[:].bitcast(FP8X4), scales[:], grouped[:].rearrange("p s m j -> p (s m j)"))
             return [(codes[:, i * P : (i + 1) * P].bitcast(FP8X4), scales[:, i * P : (i + 1) * P]) for i in range(ns)]
 
-        w1_q = quantise_weight("w1a", w1_first[:], 0, 2) + quantise_weight("w1b", w1_first[:], 2, 4)
+        w1_q = quantise_weight("w1a", w1_first[:], 0, 2, AT_W1_ROUNDED) + quantise_weight("w1b", w1_first[:], 2, 4)
 
         v_w = []
         for c in range(S // BANK):
-            t = keep.tile([P, BANK], U32, name="v_w%d" % c, align_bytes=64)
-            nc.vector.tensor_copy(t[:], tab_w[:].bitcast(U32).indirect(offs_t[:, 32 * c : 32 * (c + 1)]))
-            v_w.append(t)
+            if c == 2:
+                picked_w = place("v_w2", [P, BANK], U32, AT_W1_ROUNDED)
+            else:
+                picked_w = keep.tile([P, BANK], U32, name="v_w%d" % c, align_bytes=64)
+            entries = offs_t[:, c * BANK // 16 : (c + 1) * BANK // 16]
+            nc.vector.tensor_copy(picked_w[:], tab_w[:].bitcast(U32).indirect(entries))
+            v_w.append(picked_w)
 
-        w1_second = keep.tile([P, 4, 512], F32, name="w1_second", tag="raw8k")
-        nc.sync.dma_start(w1_second[:], w1[:, 512:1024].rearrange("(p j) c -> p j c", j=4))
+        w1_second = keep.tile([P, 4, PASS], F32, name="w1_second", tag="w1_raw")
+        nc.sync.dma_start(w1_second[:], w1[:, PASS : 2 * PASS].rearrange("(p j) c -> p j c", j=4))
         for q in range(4):
             nc.sync.dma_start(
                 w4s_raw[32 * q : 32 * q + 8, :].bitcast(I32), w4_scales[:, 4 * q : 4 * q + 4, :].bitcast(I32)
@@ -101,15 +127,15 @@ def tile_list_spatter_pair_features_kernel(
                 w2s_raw[32 * q : 32 * q + 4, :].bitcast(I32).rearrange("r (a c) -> r a c", a=2),
                 w2_scales[:, 4 * q : 4 * q + 4, :].bitcast(I32).rearrange("a r c -> r a c"),
             )
-        w2_raw = over.tile([P, 2, M // 2], I32, name="w2_raw", align_bytes=64, offset=12288)
+        w2_raw = place("w2_raw", [P, 2, M // 2], I32, AT_PICKED_SCALES)
         nc.sync.dma_start(w2_raw[:], w2_words.rearrange("a p c -> p a c").bitcast(I32))
-        w3_raw = keep.tile([P, 4, N], F32, name="w3_raw", tag="raw16k")
+        w3_raw = place("w3_raw", [P, 4, N], F32, AT_TAB_WORDS)
         w3_rows = w3.rearrange("(q t e) n -> e q t n", t=4, e=4)
         for e in range(4):
             nc.sync.dma_start(w3_raw[e:P:4, :, :], w3_rows[e])
-        gain2_t = over.tile([P, 4], F32, name="gain2_t", align_bytes=64, offset=2112)
+        gain2_t = place("gain2_t", [P, 4], F32, AT_GAIN2)
         gain2_rows = gain2.rearrange("(q t e) -> e q t", t=4, e=4)
-        with nc.allow_non_contiguous_dma(reason="one gain for each partition and word byte"):
+        with nc.allow_non_contiguous_dma(reason="one gain for each partition and byte of the word"):
             for e in range(4):
                 nc.sync.dma_start(gain2_t[e:P:4, :], gain2_rows[e])
 
@@ -119,43 +145,69 @@ def tile_list_spatter_pair_features_kernel(
             w4_raw[:].rearrange("p a (g m i s) -> p (a g) m s i", s=4, m=P // 4, i=4),
         )
 
+        tanh_rows = {}
         a1 = []
         ref = [keep.tile([P, 4, KEPT], F32, name="ref%d" % a) for a in range(2)]
 
-        tanh_rows = {}
-
         def first_product(s):
-            h = ring.tile([P, S], F32, name="h", bufs=3)
+            rows = ring.tile([P, S], F32, name="tanh_rows", bufs=AHEAD + 1)
             for c in range(S // BANK):
-                acc = psum.tile([P, BANK], F32, name="h_acc%d" % c, offset=2048 * c)
+                acc = psum.tile([P, BANK], F32, name="h_acc%d" % c, offset=BANK_BYTES * c)
                 nc.tensor.matmul_mx(
                     acc[:], lhsT=w1_q[s][0], lhsT_scale=w1_q[s][1],
                     rhs=v_w[c][:].bitcast(FP8X4), rhs_scale=v_s[:, c * BANK : (c + 1) * BANK], start=True, stop=True,
                 )
-                nc.scalar.activation(h[:, c * BANK : (c + 1) * BANK], acc[:], ACT.Tanh)
-            tanh_rows[s] = h
+                nc.scalar.activation(rows[:, c * BANK : (c + 1) * BANK], acc[:], ACT.Tanh)
+            tanh_rows[s] = rows
 
-        def first_stage(s):
+        def pair_up(s):
             a, t = divmod(s, 4)
-            h = tanh_rows[s]
-            g2 = ring.tile([P, PAIRS], F32, name="g2")
-            nc.vector.tensor_copy(g2[:], h[:].indirect(pos2_t[:]))
-            g4 = ring.tile([P, KEPT], F32, name="g4")
-            nc.vector.tensor_copy(g4[:], h[:].indirect(pos4_t[:]))
+            rows = tanh_rows[s]
+            second = ring.tile([P, PAIRS], F32, name="second")
+            nc.vector.tensor_copy(second[:], rows[:].indirect(pos2_t[:]))
+            drops = ring.tile([P, KEPT], F32, name="drops")
+            nc.vector.tensor_copy(drops[:], rows[:].indirect(pos4_t[:]))
             diff = ring.tile([P, PAIRS], F32, name="diff")
-            nc.vector.tensor_tensor(diff[:], h[:].indirect(pos1_t[:]), g2[:], ALU.subtract)
-            if s + 2 < 8:
-                first_product(s + 2)
-            nc.scalar.activation(ref[a][:, t, :], g4[:], ACT.Copy, scale=gain_t[:, a, t : t + 1])
-            d = keep.tile([P, PAIRS], F32, name="a1_%d" % s)
-            nc.scalar.activation(d[:], diff[:], ACT.Copy, scale=gain_t[:, a, t : t + 1])
-            a1.append(d)
+            nc.vector.tensor_tensor(diff[:], rows[:].indirect(pos1_t[:]), second[:], ALU.subtract)
+            if s + AHEAD < SLICES:
+                first_product(s + AHEAD)
+            nc.scalar.activation(ref[a][:, t, :], drops[:], ACT.Copy, scale=gain_t[:, a, t : t + 1])
+            pairs = keep.tile([P, PAIRS], F32, name="a1_%d" % s)
+            nc.scalar.activation(pairs[:], diff[:], ACT.Copy, scale=gain_t[:, a, t : t + 1])
+            a1.append(pairs)
 
-        first_product(0)
-        first_product(1)
-        first_stage(0)
+        def bound_pairs(a, c0, width):
+            picked = keep.tile([P, 4 * width], F32, name="picked%d" % a)
+            for t in range(4):
+                nc.vector.tensor_copy(
+                    picked[:, t * width : (t + 1) * width],
+                    a1[4 * a + t][:].indirect(pos3_t[:, c0 // 16 : (c0 + width) // 16]),
+                )
+            woven = ring.tile([P, 4 * width], BF16, name="woven%d" % a, align_bytes=64, bufs=1 + a)
+            dst = woven[:].rearrange("p (c i t) -> p c t i", i=4, t=4)
+            bound = ref[a][:, :, c0 : c0 + width]
+            if a == 0:
+                plain = keep.tile([P, 4, width], BF16, name="a2_plain")
+                nc.vector.tensor_tensor(plain[:], picked[:].rearrange("p (t c) -> p t c", t=4), bound, ALU.min)
+                nc.scalar.copy(dst, plain[:].rearrange("p t (c i) -> p c t i", i=4))
+            else:
+                nc.vector.tensor_tensor(
+                    dst, picked[:].rearrange("p (t c i) -> p c t i", t=4, i=4),
+                    bound.rearrange("p t (c i) -> p c t i", i=4), ALU.min,
+                )
+            return woven
+
+        def quantise_pairs(a, width, woven):
+            codes = ring.tile([P, width], U32, name="a2_c%d" % a, align_bytes=64)
+            scales = ring.tile([P, width], U8, name="a2_s%d" % a, align_bytes=64)
+            nc.vector.quantize_mx(codes[:].bitcast(FP8X4), scales[:], woven[:])
+            return codes, scales
+
+        for s in range(AHEAD):
+            first_product(s)
+        pair_up(0)
         w1_q += quantise_weight("w1c", w1_second[:], 0, 4)
-        first_stage(1)
+        pair_up(1)
 
         w4_s = keep.tile([P, N], U8, name="w4_s", align_bytes=64)
         nc.vector.tensor_copy(
@@ -172,61 +224,42 @@ def tile_list_spatter_pair_features_kernel(
             w2_s[:].bitcast(I32).rearrange("p (a t q) -> p a t q", a=2, t=4),
             w2s_raw[:].bitcast(I32).rearrange("p (a q t) -> p a t q", a=2, t=4),
         )
-        first_stage(2)
-        w3_q = quantise_weight("w3a", w3_raw[:, :, 0:512], 0, 4)
-        first_stage(3)
-        w3_q += quantise_weight("w3b", w3_raw[:, :, 512:1024], 0, 4)
+
+        pair_up(2)
+        w3_q = quantise_weight("w3a", w3_raw[:, :, 0:PASS], 0, 4)
+        pair_up(3)
+        w3_q += quantise_weight("w3b", w3_raw[:, :, PASS : 2 * PASS], 0, 4)
+        pair_up(4)
+
+        low_woven = bound_pairs(0, 0, KEPT)
+        pair_up(5)
+        low_c, low_s = quantise_pairs(0, KEPT, low_woven)
+        pair_up(6)
+        pair_up(7)
 
         y_scales = keep.tile([P, 2, KEPT], U8, name="y_scales", align_bytes=64)
         out_rows = out_0.rearrange("(g p t) j -> g p t j", g=2, t=4)
         out_words = out_1.rearrange("g p m t -> p g (m t)").bitcast(I32)
-
-        d_acc, y_acc, d_t = {}, {}, {}
-
-        def bound_pairs(a, c0, width, buf):
-            for t in range(4):
-                nc.vector.tensor_copy(
-                    buf[:, t * width : (t + 1) * width],
-                    a1[4 * a + t][:].indirect(pos3_t[:, c0 // 16 : (c0 + width) // 16]),
-                )
-            picked = buf[:].rearrange("p (t c i) -> p c t i", t=4, i=4)
-            bound = ref[a][:, :, c0 : c0 + width].rearrange("p t (c i) -> p c t i", i=4)
-            woven = ring.tile([P, 4 * width], BF16, name="woven%d" % a, align_bytes=64, bufs=1 + a)
-            dst = woven[:].rearrange("p (c i t) -> p c t i", i=4, t=4)
-            if a == 1:
-                nc.vector.tensor_tensor(dst, picked, bound, ALU.min)
-            else:
-                a2 = keep.tile([P, 4, width], BF16, name="a2")
-                nc.vector.tensor_tensor(
-                    a2[:], buf[:].rearrange("p (t c) -> p t c", t=4), ref[a][:, :, c0 : c0 + width], ALU.min
-                )
-                nc.scalar.copy(dst, a2[:].rearrange("p t (c i) -> p c t i", i=4))
-            return woven[:]
-
-        def quantise_pairs(a, width, woven):
-            codes = ring.tile([P, width], U32, name="qa_c%d" % a, align_bytes=64, bufs=1 + a)
-            scales = ring.tile([P, width], U8, name="qa_s%d" % a, align_bytes=64, bufs=1 + a)
-            nc.vector.quantize_mx(codes[:].bitcast(FP8X4), scales[:], woven)
-            return codes, scales
+        d_acc, y_acc, d_tanh, y_woven = {}, {}, {}, {}
 
         def multiply_pairs(u, a, codes, scales):
             if a == 0:
-                d_acc[u] = psum.tile([P, 4, UNIT], F32, name="d_acc%d" % u, offset=2048 * (u % 2))
+                d_acc[u] = psum.tile([P, 4, UNIT], F32, name="d_acc%d" % u, offset=BANK_BYTES * (u % 2))
                 y_acc[u] = [
-                    psum.tile([P, 4, UNIT], F32, name="y_acc%d_%d" % (u, g), offset=2048 * ((2 * u + 2) % 6 + 2 + g))
+                    psum.tile([P, 4, UNIT], F32, name="y_acc%d_%d" % (u, g), offset=BANK_BYTES * (2 + 2 * ((u + 1) % 3) + g))
                     for g in range(2)
                 ]
             for t in range(4):
+                c0 = (4 * a + t) * P
                 nc.tensor.matmul_mx(
                     d_acc[u][:, t, :],
-                    lhsT=w2_c[:, (4 * a + t) * 256 : (4 * a + t + 1) * 256].bitcast(FP4X4),
-                    lhsT_scale=w2_s[:, (4 * a + t) * P : (4 * a + t + 1) * P],
+                    lhsT=w2_c[:, 2 * c0 : 2 * (c0 + P)].bitcast(FP4X4), lhsT_scale=w2_s[:, c0 : c0 + P],
                     rhs=codes.bitcast(FP8X4), rhs_scale=scales,
                     start=(a == 0 and t == 0), stop=(a == 1 and t == 3),
                 )
             if a == 1:
-                d_t[u] = ring.tile([P, UNIT, 4], F32, name="d_t")
-                nc.scalar.activation(d_t[u][:], d_acc[u][:].rearrange("p t c -> p c t"), ACT.Tanh)
+                d_tanh[u] = ring.tile([P, UNIT, 4], F32, name="d_tanh")
+                nc.scalar.activation(d_tanh[u][:], d_acc[u][:].rearrange("p t c -> p c t"), ACT.Tanh)
             for g in range(2):
                 for t in range(4):
                     c0 = (4 * g + t) * P
@@ -239,59 +272,47 @@ def tile_list_spatter_pair_features_kernel(
                     )
 
         def second_stage(u):
-            d_i = ring.tile([P, UNIT, 4], BF16, name="d_i", align_bytes=64)
+            d_woven = ring.tile([P, UNIT, 4], BF16, name="d_woven", align_bytes=64)
             nc.vector.tensor_tensor(
-                d_i[:], d_t[u][:],
-                gain2_t[:].unsqueeze(1).to_broadcast([P, UNIT, 4]), ALU.mult,
+                d_woven[:], d_tanh[u][:], gain2_t[:].unsqueeze(1).to_broadcast([P, UNIT, 4]), ALU.mult
             )
-            qd_c = ring.tile([P, UNIT], U32, name="qd_c", align_bytes=64)
-            qd_s = ring.tile([P, UNIT], U8, name="qd_s", align_bytes=64)
-            nc.vector.quantize_mx(qd_c[:].bitcast(FP8X4), qd_s[:], d_i[:].rearrange("p c t -> p (c t)"))
+            d_c = ring.tile([P, UNIT], U32, name="d_c", align_bytes=64)
+            d_s = ring.tile([P, UNIT], U8, name="d_s", align_bytes=64)
+            nc.vector.quantize_mx(d_c[:].bitcast(FP8X4), d_s[:], d_woven[:].rearrange("p c t -> p (c t)"))
             for g in range(2):
                 for t in range(4):
                     nc.tensor.matmul_mx(
                         y_acc[u][g][:, t, :], lhsT=w3_q[4 * g + t][0], lhsT_scale=w3_q[4 * g + t][1],
-                        rhs=qd_c[:].bitcast(FP8X4), rhs_scale=qd_s[:], start=False, stop=(t == 3),
+                        rhs=d_c[:].bitcast(FP8X4), rhs_scale=d_s[:], start=False, stop=(t == 3),
                     )
-
-        y_i = {}
 
         def empty_y(u):
             for g in range(2):
-                y_i[u, g] = ring.tile([P, 4 * UNIT], BF16, name="y_i%d" % g, align_bytes=64)
-                dst = y_i[u, g][:].rearrange("p (c t) -> p c t", t=4)
+                y_woven[u, g] = ring.tile([P, 4 * UNIT], BF16, name="y_woven%d" % g, align_bytes=64)
+                dst = y_woven[u, g][:].rearrange("p (c t) -> p c t", t=4)
                 if 2 * u + g >= 2 * UNITS - 3:
                     nc.vector.tensor_copy(dst, y_acc[u][g][:].rearrange("p t c -> p c t"))
                 else:
                     nc.scalar.copy(dst, y_acc[u][g][:].rearrange("p t c -> p c t"))
             for g in range(2):
-                y_f = ring.tile([P, 4, UNIT], F32, name="y_f%d" % g)
+                y_f32 = ring.tile([P, 4, UNIT], F32, name="y_f32_%d" % g)
                 if 2 * u + g == 2 * UNITS - 1:
-                    nc.vector.tensor_copy(y_f[:], y_acc[u][g][:])
+                    nc.vector.tensor_copy(y_f32[:], y_acc[u][g][:])
                 else:
-                    nc.scalar.copy(y_f[:], y_acc[u][g][:])
-                nc.sync.dma_start(out_rows[g][:, :, u * UNIT : (u + 1) * UNIT], y_f[:])
+                    nc.scalar.copy(y_f32[:], y_acc[u][g][:])
+                nc.sync.dma_start(out_rows[g][:, :, u * UNIT : (u + 1) * UNIT], y_f32[:])
 
         def quantise_y(u):
             cols = slice(u * UNIT, (u + 1) * UNIT)
             y_codes = ring.tile([P, 2, UNIT], I32, name="y_codes", align_bytes=64)
             for g in range(2):
-                nc.vector.quantize_mx(y_codes[:, g, :].bitcast(FP8X4), y_scales[:, g, cols], y_i[u, g][:])
+                nc.vector.quantize_mx(y_codes[:, g, :].bitcast(FP8X4), y_scales[:, g, cols], y_woven[u, g][:])
             nc.sync.dma_start(out_words[:, :, cols], y_codes[:])
 
-        first_stage(4)
-        wide_buf = keep.tile([P, 4 * KEPT], F32, name="wide_buf", align_bytes=64)
-        wide = bound_pairs(0, 0, KEPT, wide_buf)
-        first_stage(5)
-        low_c, low_s = quantise_pairs(0, KEPT, wide)
-        first_stage(6)
-        first_stage(7)
-        unit_buf = keep.tile([P, 4 * UNIT], F32, name="unit_buf", align_bytes=64)
         for u in range(UNITS):
             cols = slice(u * UNIT, (u + 1) * UNIT)
             multiply_pairs(u, 0, low_c[:, cols], low_s[:, cols])
-            woven = bound_pairs(1, u * UNIT, UNIT, unit_buf)
-            high_c, high_s = quantise_pairs(1, UNIT, woven)
+            high_c, high_s = quantise_pairs(1, UNIT, bound_pairs(1, u * UNIT, UNIT))
             multiply_pairs(u, 1, high_c[:], high_s[:])
             if u >= 1:
                 second_stage(u - 1)
@@ -305,8 +326,8 @@ def tile_list_spatter_pair_features_kernel(
             quantise_y(u)
 
         for q in range(4):
-            eng = nc.scalar if q % 2 else nc.sync
-            eng.dma_start(
+            queue = nc.scalar if q % 2 else nc.sync
+            queue.dma_start(
                 out_2[:, 4 * q : 4 * q + 4, :].bitcast(I32).rearrange("g r c -> r g c"),
                 y_scales[32 * q : 32 * q + 4, :, :].bitcast(I32),
             )

from contextlib import ExitStack

import concourse.mybir as mybir

F32 = mybir.dt.float32
BF16 = mybir.dt.bfloat16
I32 = mybir.dt.int32
U32 = mybir.dt.uint32
U16 = mybir.dt.uint16
U8 = mybir.dt.uint8
FP8X4 = mybir.dt.float8_e4m3fn_x4
FP4X4 = mybir.dt.float4_e2m1fn_x4
ACT = mybir.ActivationFunctionType
ALU = mybir.AluOpType

T, S, PAIRS, KEPT = 4096, 2048, 1024, 512
K, H, M, N = 512, 1024, 512, 1024
P = 128
PASS = 512
BANK = 512
BANK_BYTES = 4 * BANK
SLICES = H // P
AHEAD = 2
UNIT = 128
UNITS = KEPT // UNIT
SCALE_ROW0 = P - 16
FLOPS = 2 * (K * H * S + H * M * KEPT + M * N * KEPT + H * N * KEPT)

AT_TAB_SCALES = 0
AT_W4_SCALES_RAW = 0
AT_W2_SCALES_RAW = 1024
AT_GAIN = 2048
AT_GAIN2 = 2112
AT_W4_RAW = T - 64
AT_PICKED_SCALES = 12288
AT_TAB_WORDS = 14336
AT_W1_ROUNDED = 30720


def tile_list_spatter_pair_features_kernel(
    tc, tab_words, tab_scales, offs, pos1, pos2, pos3, pos4, w1, gain, w2_words, w2_scales, gain2, w3,
    w4_words, w4_scales, out_0, out_1, out_2,
):
    nc = tc.nc
    with ExitStack() as ctx:
        keep = ctx.enter_context(tc.tile_pool(name="keep", bufs=1))
        ring = ctx.enter_context(tc.tile_pool(name="ring", bufs=2))
        placed = ctx.enter_context(tc.tile_pool(name="placed", bufs=1))
        psum = ctx.enter_context(tc.psum_pool(name="psum", bufs=1))

        def place(name, shape, dtype, at):
            return placed.tile(shape, dtype, name=name, align_bytes=64, offset=at)

        def load_list(name, src):
            t = keep.tile(list(src.shape), U16, name=name)
            nc.sync.dma_start(t[:], src)
            return t

        tab_s = place("tab_s", [P, T], U8, AT_TAB_SCALES)
        nc.sync.dma_start(tab_s[SCALE_ROW0:P, :].bitcast(I32), tab_scales[0].bitcast(I32))
        offs_t = load_list("offs_t", offs)
        nc.vector.memset(tab_s[0:96, :].bitcast(I32), 0)
        nc.gpsimd.memset(tab_s[96:SCALE_ROW0, :].bitcast(I32), 0)
        v_s = keep.tile([P, S], U8, name="v_s", align_bytes=64)
        nc.gpsimd.memset(v_s[:].bitcast(I32), 0)
        tab_w = place("tab_w", [P, T], I32, AT_TAB_WORDS)
        nc.sync.dma_start(tab_w[:], tab_words[0].rearrange("p t i -> p (t i)").bitcast(I32))
        pos2_t = load_list("pos2_t", pos2)
        w1_first = keep.tile([P, 4, PASS], F32, name="w1_first", tag="w1_raw")
        nc.sync.dma_start(w1_first[:], w1[:, 0:PASS].rearrange("(p j) c -> p j c", j=4))
        pos4_t = load_list("pos4_t", pos4)
        pos1_t = load_list("pos1_t", pos1)
        pos3_t = load_list("pos3_t", pos3)

        picked_s = place("picked_s", [P, S], U8, AT_PICKED_SCALES)
        nc.vector.tensor_copy(picked_s[:], tab_s[:].indirect(offs_t[:]))
        for q in range(4):
            nc.sync.dma_start(
                v_s[32 * q : 32 * q + 4, :].bitcast(I32),
                picked_s[SCALE_ROW0 + 4 * q : SCALE_ROW0 + 4 * q + 4, :].bitcast(I32),
            )

        w4_raw = place("w4_raw", [P, 2, N], I32, AT_W4_RAW)
        nc.sync.dma_start(w4_raw[:], w4_words.rearrange("a p c i -> p a (c i)").bitcast(I32))
        gain_t = place("gain_t", [P, 2, 4], F32, AT_GAIN)
        nc.sync.dma_start(gain_t[:], gain.rearrange("(a p t) -> p a t", a=2, t=4))
        w4s_raw = place("w4s_raw", [P, N], U8, AT_W4_SCALES_RAW)
        nc.gpsimd.memset(w4s_raw[:].bitcast(I32), 0)
        w2s_raw = place("w2s_raw", [P, 2 * M], U8, AT_W2_SCALES_RAW)
        nc.gpsimd.memset(w2s_raw[:].bitcast(I32), 0)

        def quantise_weight(name, raw, s0, s1, at=None):
            ns = s1 - s0
            if at is None:
                grouped = keep.tile([P, ns, P, 4], BF16, name=name + "_bf", align_bytes=64)
            else:
                grouped = place(name + "_bf", [P, ns, P, 4], BF16, at)
            nc.scalar.copy(
                grouped[:].rearrange("p (r i) m j -> p r m j i", i=2),
                raw.rearrange("p j (m r i) -> p r m j i", r=2, i=2)[:, s0 // 2 : s1 // 2],
            )
            codes = keep.tile([P, ns * P], U32, name=name + "_c", align_bytes=64)
            scales = keep.tile([P, ns * P], U8, name=name + "_s", align_bytes=64)
            nc.vector.quantize_mx(codes[:].bitcast(FP8X4), scales[:], grouped[:].rearrange("p s m j -> p (s m j)"))
            return [(codes[:, i * P : (i + 1) * P].bitcast(FP8X4), scales[:, i * P : (i + 1) * P]) for i in range(ns)]

        w1_q = quantise_weight("w1a", w1_first[:], 0, 2, AT_W1_ROUNDED) + quantise_weight("w1b", w1_first[:], 2, 4)

        v_w = []
        for c in range(S // BANK):
            if c == 2:
                picked_w = place("v_w2", [P, BANK], U32, AT_W1_ROUNDED)
            else:
                picked_w = keep.tile([P, BANK], U32, name="v_w%d" % c, align_bytes=64)
            entries = offs_t[:, c * BANK // 16 : (c + 1) * BANK // 16]
            nc.vector.tensor_copy(picked_w[:], tab_w[:].bitcast(U32).indirect(entries))
            v_w.append(picked_w)

        w1_second = keep.tile([P, 4, PASS], F32, name="w1_second", tag="w1_raw")
        nc.sync.dma_start(w1_second[:], w1[:, PASS : 2 * PASS].rearrange("(p j) c -> p j c", j=4))
        for q in range(4):
            nc.sync.dma_start(
                w4s_raw[32 * q : 32 * q + 8, :].bitcast(I32), w4_scales[:, 4 * q : 4 * q + 4, :].bitcast(I32)
            )
        for q in range(4):
            nc.sync.dma_start(
                w2s_raw[32 * q : 32 * q + 4, :].bitcast(I32).rearrange("r (a c) -> r a c", a=2),
                w2_scales[:, 4 * q : 4 * q + 4, :].bitcast(I32).rearrange("a r c -> r a c"),
            )
        w2_raw = place("w2_raw", [P, 2, M // 2], I32, AT_PICKED_SCALES)
        nc.sync.dma_start(w2_raw[:], w2_words.rearrange("a p c -> p a c").bitcast(I32))
        w3_raw = place("w3_raw", [P, 4, N], F32, AT_TAB_WORDS)
        w3_rows = w3.rearrange("(q t e) n -> e q t n", t=4, e=4)
        for e in range(4):
            nc.sync.dma_start(w3_raw[e:P:4, :, :], w3_rows[e])
        gain2_t = place("gain2_t", [P, 4], F32, AT_GAIN2)
        gain2_rows = gain2.rearrange("(q t e) -> e q t", t=4, e=4)
        with nc.allow_non_contiguous_dma(reason="one gain for each partition and byte of the word"):
            for e in range(4):
                nc.sync.dma_start(gain2_t[e:P:4, :], gain2_rows[e])

        w4_c = keep.tile([P, 2 * N], I32, name="w4_c", align_bytes=64)
        nc.vector.tensor_copy(
            w4_c[:].rearrange("p (b s m i) -> p b m s i", s=4, m=P // 4, i=4),
            w4_raw[:].rearrange("p a (g m i s) -> p (a g) m s i", s=4, m=P // 4, i=4),
        )

        tanh_rows = {}
        a1 = []
        ref = [keep.tile([P, 4, KEPT], F32, name="ref%d" % a) for a in range(2)]

        def first_product(s):
            rows = ring.tile([P, S], F32, name="tanh_rows", bufs=AHEAD + 1)
            for c in range(S // BANK):
                acc = psum.tile([P, BANK], F32, name="h_acc%d" % c, offset=BANK_BYTES * c)
                nc.tensor.matmul_mx(
                    acc[:], lhsT=w1_q[s][0], lhsT_scale=w1_q[s][1],
                    rhs=v_w[c][:].bitcast(FP8X4), rhs_scale=v_s[:, c * BANK : (c + 1) * BANK], start=True, stop=True,
                )
                nc.scalar.activation(rows[:, c * BANK : (c + 1) * BANK], acc[:], ACT.Tanh)
            tanh_rows[s] = rows

        def pair_up(s):
            a, t = divmod(s, 4)
            rows = tanh_rows[s]
            second = ring.tile([P, PAIRS], F32, name="second")
            nc.vector.tensor_copy(second[:], rows[:].indirect(pos2_t[:]))
            drops = ring.tile([P, KEPT], F32, name="drops")
            nc.vector.tensor_copy(drops[:], rows[:].indirect(pos4_t[:]))
            diff = ring.tile([P, PAIRS], F32, name="diff")
            nc.vector.tensor_tensor(diff[:], rows[:].indirect(pos1_t[:]), second[:], ALU.subtract)
            if s + AHEAD < SLICES:
                first_product(s + AHEAD)
            nc.scalar.activation(ref[a][:, t, :], drops[:], ACT.Copy, scale=gain_t[:, a, t : t + 1])
            pairs = keep.tile([P, PAIRS], F32, name="a1_%d" % s)
            nc.scalar.activation(pairs[:], diff[:], ACT.Copy, scale=gain_t[:, a, t : t + 1])
            a1.append(pairs)

        def bound_pairs(a, c0, width):
            picked = keep.tile([P, 4 * width], F32, name="picked%d" % a)
            for t in range(4):
                nc.vector.tensor_copy(
                    picked[:, t * width : (t + 1) * width],
                    a1[4 * a + t][:].indirect(pos3_t[:, c0 // 16 : (c0 + width) // 16]),
                )
            woven = ring.tile([P, 4 * width], BF16, name="woven%d" % a, align_bytes=64, bufs=1 + a)
            dst = woven[:].rearrange("p (c i t) -> p c t i", i=4, t=4)
            bound = ref[a][:, :, c0 : c0 + width]
            if a == 0:
                plain = keep.tile([P, 4, width], BF16, name="a2_plain")
                nc.vector.tensor_tensor(plain[:], picked[:].rearrange("p (t c) -> p t c", t=4), bound, ALU.min)
                nc.scalar.copy(dst, plain[:].rearrange("p t (c i) -> p c t i", i=4))
            else:
                nc.vector.tensor_tensor(
                    dst, picked[:].rearrange("p (t c i) -> p c t i", t=4, i=4),
                    bound.rearrange("p t (c i) -> p c t i", i=4), ALU.min,
                )
            return woven

        def quantise_pairs(a, width, woven):
            codes = ring.tile([P, width], U32, name="a2_c%d" % a, align_bytes=64)
            scales = ring.tile([P, width], U8, name="a2_s%d" % a, align_bytes=64)
            nc.vector.quantize_mx(codes[:].bitcast(FP8X4), scales[:], woven[:])
            return codes, scales

        for s in range(AHEAD):
            first_product(s)
        pair_up(0)
        w1_q += quantise_weight("w1c", w1_second[:], 0, 4)
        pair_up(1)

        w4_s = keep.tile([P, N], U8, name="w4_s", align_bytes=64)
        nc.vector.tensor_copy(
            w4_s[:].rearrange("p (g s m) -> p g s m", s=4, m=P),
            w4s_raw[:].rearrange("p (g m s) -> p g s m", s=4, m=P),
        )
        w2_c = keep.tile([P, 2 * 2 * M], U8, name="w2_c", align_bytes=64)
        nc.vector.tensor_copy(
            w2_c[:].bitcast(I32).rearrange("p (a t q e) -> p a t q e", a=2, t=4, e=2),
            w2_raw[:].rearrange("p a (q t e) -> p a t q e", t=4, e=2),
        )
        w2_s = keep.tile([P, 2 * M], U8, name="w2_s", align_bytes=64)
        nc.vector.tensor_copy(
            w2_s[:].bitcast(I32).rearrange("p (a t q) -> p a t q", a=2, t=4),
            w2s_raw[:].bitcast(I32).rearrange("p (a q t) -> p a t q", a=2, t=4),
        )

        pair_up(2)
        w3_q = quantise_weight("w3a", w3_raw[:, :, 0:PASS], 0, 4)
        pair_up(3)
        w3_q += quantise_weight("w3b", w3_raw[:, :, PASS : 2 * PASS], 0, 4)
        pair_up(4)

        low_woven = bound_pairs(0, 0, KEPT)
        pair_up(5)
        low_c, low_s = quantise_pairs(0, KEPT, low_woven)
        pair_up(6)
        pair_up(7)

        y_scales = keep.tile([P, 2, KEPT], U8, name="y_scales", align_bytes=64)
        out_rows = out_0.rearrange("(g p t) j -> g p t j", g=2, t=4)
        out_words = out_1.rearrange("g p m t -> p g (m t)").bitcast(I32)
        d_acc, y_acc, d_tanh, y_woven = {}, {}, {}, {}

        def multiply_pairs(u, a, codes, scales):
            if a == 0:
                d_acc[u] = psum.tile([P, 4, UNIT], F32, name="d_acc%d" % u, offset=BANK_BYTES * (u % 2))
                y_acc[u] = [
                    psum.tile([P, 4, UNIT], F32, name="y_acc%d_%d" % (u, g), offset=BANK_BYTES * (2 + 2 * ((u + 1) % 3) + g))
                    for g in range(2)
                ]
            for t in range(4):
                c0 = (4 * a + t) * P
                nc.tensor.matmul_mx(
                    d_acc[u][:, t, :],
                    lhsT=w2_c[:, 2 * c0 : 2 * (c0 + P)].bitcast(FP4X4), lhsT_scale=w2_s[:, c0 : c0 + P],
                    rhs=codes.bitcast(FP8X4), rhs_scale=scales,
                    start=(a == 0 and t == 0), stop=(a == 1 and t == 3),
                )
            if a == 1:
                d_tanh[u] = ring.tile([P, UNIT, 4], F32, name="d_tanh")
                nc.scalar.activation(d_tanh[u][:], d_acc[u][:].rearrange("p t c -> p c t"), ACT.Tanh)
            for g in range(2):
                for t in range(4):
                    c0 = (4 * g + t) * P
                    nc.tensor.matmul_mx(
                        y_acc[u][g][:, t, :],
                        lhsT=w4_c[:, a * N + c0 : a * N + c0 + P].bitcast(FP8X4),
                        lhsT_scale=w4_s[4 * a : P, c0 : c0 + P],
                        rhs=codes.bitcast(FP8X4), rhs_scale=scales,
                        start=(a == 0 and t == 0), stop=False,
                    )

        def second_stage(u):
            d_woven = ring.tile([P, UNIT, 4], BF16, name="d_woven", align_bytes=64)
            nc.vector.tensor_tensor(
                d_woven[:], d_tanh[u][:], gain2_t[:].unsqueeze(1).to_broadcast([P, UNIT, 4]), ALU.mult
            )
            d_c = ring.tile([P, UNIT], U32, name="d_c", align_bytes=64)
            d_s = ring.tile([P, UNIT], U8, name="d_s", align_bytes=64)
            nc.vector.quantize_mx(d_c[:].bitcast(FP8X4), d_s[:], d_woven[:].rearrange("p c t -> p (c t)"))
            for g in range(2):
                for t in range(4):
                    nc.tensor.matmul_mx(
                        y_acc[u][g][:, t, :], lhsT=w3_q[4 * g + t][0], lhsT_scale=w3_q[4 * g + t][1],
                        rhs=d_c[:].bitcast(FP8X4), rhs_scale=d_s[:], start=False, stop=(t == 3),
                    )

        def empty_y(u):
            for g in range(2):
                y_woven[u, g] = ring.tile([P, 4 * UNIT], BF16, name="y_woven%d" % g, align_bytes=64)
                dst = y_woven[u, g][:].rearrange("p (c t) -> p c t", t=4)
                if 2 * u + g >= 2 * UNITS - 3:
                    nc.vector.tensor_copy(dst, y_acc[u][g][:].rearrange("p t c -> p c t"))
                else:
                    nc.scalar.copy(dst, y_acc[u][g][:].rearrange("p t c -> p c t"))
            for g in range(2):
                y_f32 = ring.tile([P, 4, UNIT], F32, name="y_f32_%d" % g)
                if 2 * u + g == 2 * UNITS - 1:
                    nc.vector.tensor_copy(y_f32[:], y_acc[u][g][:])
                else:
                    nc.scalar.copy(y_f32[:], y_acc[u][g][:])
                nc.sync.dma_start(out_rows[g][:, :, u * UNIT : (u + 1) * UNIT], y_f32[:])

        def quantise_y(u):
            cols = slice(u * UNIT, (u + 1) * UNIT)
            y_codes = ring.tile([P, 2, UNIT], I32, name="y_codes", align_bytes=64)
            for g in range(2):
                nc.vector.quantize_mx(y_codes[:, g, :].bitcast(FP8X4), y_scales[:, g, cols], y_woven[u, g][:])
            nc.sync.dma_start(out_words[:, :, cols], y_codes[:])

        for u in range(UNITS):
            cols = slice(u * UNIT, (u + 1) * UNIT)
            multiply_pairs(u, 0, low_c[:, cols], low_s[:, cols])
            high_c, high_s = quantise_pairs(1, UNIT, bound_pairs(1, u * UNIT, UNIT))
            multiply_pairs(u, 1, high_c[:], high_s[:])
            if u >= 1:
                second_stage(u - 1)
            if u >= 2:
                empty_y(u - 2)
                quantise_y(u - 2)
        second_stage(UNITS - 1)
        for u in range(UNITS - 2, UNITS):
            empty_y(u)
        for u in range(UNITS - 2, UNITS):
            quantise_y(u)

        for q in range(4):
            queue = nc.scalar if q % 2 else nc.sync
            queue.dma_start(
                out_2[:, 4 * q : 4 * q + 4, :].bitcast(I32).rearrange("g r c -> r g c"),
                y_scales[32 * q : 32 * q + 4, :, :].bitcast(I32),
            )
